import numpy as np
import ml_dtypes


def mxq(x, axis, fmt="e4m3"):
    dtype, down = {"e4m3": (ml_dtypes.float8_e4m3fn, 7), "e5m2": (ml_dtypes.float8_e5m2, 14)}[fmt]
    v = np.moveaxis(np.asarray(x, np.float32).astype(ml_dtypes.bfloat16).astype(np.float64), axis, -1)
    blocks = v.reshape(v.shape[:-1] + (-1, 32))
    amax = np.abs(blocks).max(-1, keepdims=True)
    byte = np.maximum(np.where(amax > 0, np.frexp(amax)[1] - 1 + 127, 0) - down, 1)
    scale = np.exp2(byte - 127.0)
    codes = (blocks / scale).astype(np.float32).astype(dtype).astype(np.float64)
    return np.moveaxis((codes * scale).reshape(v.shape), -1, axis)


WIDE = False


def mx_kscale(k):
    if not WIDE:
        return np.ones(k)
    levels = np.array([10, -10, 5, -5, 0])
    if k % 512:
        return np.exp2(np.random.permutation(np.resize(levels, k // 32))).repeat(32)
    a = np.empty((k // 512, 16))
    for p in range(k // 512):
        a[p, :8] = np.random.permutation(np.resize(levels, 8))
        for g in range(8):
            far = levels[np.abs(levels - a[p, g]) >= 10]
            a[p, g + 8] = far[np.random.randint(len(far))]
    return np.exp2(a.ravel()).repeat(32)


def f64(x):
    return np.asarray(x).astype(np.float64)


def striped(idx):
    return np.tile(idx.reshape(-1, 16).T, (8, 1)).astype(np.uint16)


def unstriped(offs):
    return offs[:16].T.reshape(-1).astype(np.int64)


E2M1 = np.array([0.0, 0.5, 1.0, 1.5, 2.0, 3.0, 4.0, 6.0, -0.0, -0.5, -1.0, -1.5, -2.0, -3.0, -4.0, -6.0])


def pack_weight(w, fmt):
    k, n = w.shape
    w = f64(np.asarray(w, np.float32).astype(ml_dtypes.bfloat16)).reshape(k // 32, 32, n)
    amax = np.abs(w).max(1)
    if fmt == "e4m3":
        byte = np.frexp(amax)[1] - 1 + 127 - 7
    else:
        mant, ex = np.frexp(amax / 6.0)
        byte = np.where(mant > 0.5, ex, ex - 1) + 127
    byte = np.clip(np.where(amax > 0, byte, 1), 1, 254)
    scaled = (w * np.exp2(127.0 - byte)[:, None, :]).reshape(k, n).astype(np.float32)
    by_word = np.ascontiguousarray(scaled.reshape(k // 512, 128, 4, n).transpose(0, 1, 3, 2))
    if fmt == "e4m3":
        words = by_word.astype(ml_dtypes.float8_e4m3fn).view(np.uint8)
    else:
        c = by_word.astype(ml_dtypes.float4_e2m1fn).view(np.uint8) & 0xF
        words = (c[..., 0::2] | (c[..., 1::2] << 4)).reshape(k // 512, 128, 2 * n)
    return np.ascontiguousarray(words), np.ascontiguousarray(byte.astype(np.uint8).reshape(k // 512, 16, n))


def unpack_weight(words, scales, fmt):
    g, _, n = scales.shape
    words = np.ascontiguousarray(words).reshape(g, 128, n, -1)
    if fmt == "e4m3":
        vals = words.view(ml_dtypes.float8_e4m3fn).astype(np.float64)
    else:
        nib = np.empty((g, 128, n, 4), np.uint8)
        nib[..., 0::2] = words & 0xF
        nib[..., 1::2] = words >> 4
        vals = E2M1[nib]
    vals = vals * np.repeat(np.exp2(scales.astype(np.float64) - 127.0), 8, axis=1)[..., None]
    return vals.transpose(0, 1, 3, 2).reshape(g * 512, n)


def planes(y):
    n, m = y.shape
    v = y.astype(np.float32).astype(ml_dtypes.bfloat16).astype(np.float64).reshape(n // 32, 32, m)
    top = np.abs(v).max(1)
    byte = np.clip(np.where(top > 0, np.frexp(top)[1] - 1 + 127 - 7, 1), 1, 254)
    codes = (v * np.exp2(127.0 - byte)[:, None, :]).reshape(n, m).astype(np.float32).astype(ml_dtypes.float8_e4m3fn).view(np.uint8)
    words = codes.reshape(n // 512, 128, 4, m).transpose(0, 1, 3, 2)
    return np.ascontiguousarray(words), np.ascontiguousarray(byte.astype(np.uint8).reshape(n // 512, 16, m))


def gelu(v):
    return 0.5 * v * (1.0 + np.tanh(np.sqrt(2.0 / np.pi) * (v + 0.044715 * v**3)))


D, T, E, C, H, N = 2, 512, 4, 256, 512, 512


def by_expert(wq, xq):
    return np.concatenate([wq[e].T @ xq[:, e * C:(e + 1) * C] for e in range(E)], axis=1)


def setup_inputs():
    n = np.random.standard_normal
    s = np.tile(mx_kscale(H), D)
    u = mx_kscale(H)
    slot_sub = np.random.permutation(D * T)
    x = pack_weight(n((D * H, T)) * s[:, None], "e4m3")
    w = [pack_weight(m, "e4m3") for m in n((E, H, H)) / np.sqrt(H) / s[None, :H, None] * u]
    return {
        "x_words": x[0],
        "x_scales": x[1],
        "w_words": np.stack([m[0] for m in w]),
        "w_scales": np.stack([m[1] for m in w]),
        "wm": (n((D * H, N)) / np.sqrt(D * H) / np.tile(u, D)[:, None]).astype(np.float32),
        "gate": np.tile(np.random.uniform(0.2, 1.0, E * C), (128, 1)).astype(np.float32),
        "offs": striped(slot_sub),
    }


def reference(x_words, x_scales, w_words, w_scales, wm, gate, offs):
    w = np.stack([unpack_weight(w_words[e], w_scales[e], "e4m3") for e in range(E)])
    wmq = mxq(f64(wm), 0, "e4m3")
    idx = unstriped(offs)
    x = unpack_weight(x_words, x_scales, "e4m3")
    sub = x.reshape(D, H, T).transpose(1, 0, 2).reshape(H, D * T)
    y = gelu(by_expert(w, sub[:, idx]))
    c = np.zeros((H, D * T))
    c[:, idx] = f64(gate[:1]) * y
    cq = mxq(c, 0, "e4m3").reshape(H, D, T).transpose(1, 0, 2).reshape(D * H, T)
    out_0 = wmq.T @ cq
    return (out_0,) + planes(out_0)

@@ -1,0 +1,230 @@
+from contextlib import ExitStack
+
+import concourse.mybir as mybir
+from concourse.masks import make_identity
+
+D, T, E, C, H, N = 2, 512, 4, 256, 512, 512
+P = 128
+S = E * C
+FLOPS = 2 * H * H * S + 2 * D * H * N * T
+
+F32 = mybir.dt.float32
+BF16 = mybir.dt.bfloat16
+I32 = mybir.dt.int32
+U32 = mybir.dt.uint32
+U16 = mybir.dt.uint16
+U8 = mybir.dt.uint8
+X4 = mybir.dt.float8_e4m3fn_x4
+GELU = mybir.ActivationFunctionType.Gelu_apprx_tanh
+COPY = mybir.ActivationFunctionType.Copy
+
+GATHERS = ((0, 128), (128, 256), (256, 512), (512, 1024))
+MULT = mybir.AluOpType.mult
+ADD = mybir.AluOpType.add
+TC = 128
+CHUNKS = T // TC
+
+
+def tile_moe_mhm_gelu_kernel(
+    tc, x_words, x_scales, w_words, w_scales, wm, gate, offs, out_0, out_1, out_2
+):
+    nc = tc.nc
+    with ExitStack() as ctx:
+        keep = ctx.enter_context(tc.tile_pool(name="keep", bufs=1))
+        ring = ctx.enter_context(tc.tile_pool(name="ring", bufs=3))
+        pair = ctx.enter_context(tc.tile_pool(name="pair", bufs=2))
+        acc_pool = ctx.enter_context(tc.psum_pool(name="acc", bufs=4))
+        turn_pool = ctx.enter_context(tc.psum_pool(name="turn", bufs=3))
+
+        offsets = keep.tile([P, S // 16], U16, name="offsets")
+        xw = keep.tile([P, D * T], U32, name="xw", tag="then_wm1", align_bytes=64)
+        xs = keep.tile([P, D * T], U8, name="xs", align_bytes=64)
+        ws = keep.tile([P, H], U8, name="ws", align_bytes=64)
+        w_first = keep.tile([P, H], U32, name="w_first", align_bytes=64)
+        ww = [w_first[:]]
+        gate_cols = keep.tile([P, S // P], F32, name="gate_cols")
+        wm_raw = []
+        ident = keep.tile([P, P], F32, name="ident")
+        warm_in = keep.tile([P, 1], F32, name="warm_in", tag="then_w", align_bytes=64)
+        warm_out = keep.tile([P, 1], F32, name="warm_out", tag="then_wm0", align_bytes=64)
+
+        nc.gpsimd.memset(xs[:].bitcast(I32), 0)
+        nc.gpsimd.memset(ws[:].bitcast(I32), 0)
+        nc.vector.memset(warm_in[:], 0.0)
+        nc.scalar.activation(warm_out[:], warm_in[:], GELU)
+
+        nc.sync.dma_start(offsets[:], offs)
+        nc.sync.dma_start(
+            xw[:].bitcast(I32).rearrange("p (o t) -> p o t", o=D),
+            x_words.rearrange("o p t d -> p o (t d)").bitcast(I32),
+        )
+        for q in range(4):
+            nc.sync.dma_start(
+                xs[32 * q : 32 * q + 4, :].bitcast(I32).rearrange("r (o t) -> r o t", o=D),
+                x_scales[:, 4 * q : 4 * q + 4, :].rearrange("o r t -> r o t").bitcast(I32),
+            )
+
+        def load_w(e):
+            nc.sync.dma_start(ww[e].bitcast(I32), w_words[e, 0].rearrange("p l d -> p (l d)").bitcast(I32))
+
+        def load_wm(o):
+            wm_raw.append(keep.tile([P, 4, N], F32, name="wm_raw%d" % o, tag="then_wm%d" % o, align_bytes=64))
+            nc.sync.dma_start(wm_raw[o][:], wm[o * H : (o + 1) * H, :].rearrange("(p j) n -> p j n", j=4))
+
+        load_w(0)
+        for q in range(4):
+            (nc.sync if q < 3 else nc.gpsimd).dma_start(
+                ws[32 * q : 32 * q + 16, :].bitcast(I32),
+                w_scales[:, 0, 4 * q : 4 * q + 4, :].bitcast(I32),
+            )
+
+        make_identity(nc, ident[:])
+        gate_rows = keep.tile([P, P], F32, name="gate_rows", tag="then_wm0", align_bytes=64)
+        nc.sync.dma_start(gate_rows[:], gate[0:16, :].rearrange("a (j c) -> (a j) c", c=P))
+        w_rest = keep.tile([P, (E - 1) * H], U32, name="w_rest", tag="then_w", align_bytes=64)
+        for e in range(1, E):
+            ww.append(w_rest[:, (e - 1) * H : e * H])
+            load_w(e)
+
+        gathered = {}
+
+        def gather(a, b):
+            xg = pair.tile([P, b - a], U32, name="xg", align_bytes=64)
+            sg = pair.tile([P, b - a], U8, name="sg", align_bytes=64)
+            nc.vector.tensor_copy(xg[:], xw[:].indirect(offsets[:, a // 16 : b // 16]))
+            nc.vector.tensor_copy(sg[:], xs[:].indirect(offsets[:, a // 16 : b // 16]))
+            for first in range(a, b, P):
+                part = slice(first - a, first - a + P)
+                gathered.setdefault(first // P, (xg[:, part], sg[:, part]))
+
+        for a, b in GATHERS[:2]:
+            gather(a, b)
+
+        gate_turned = turn_pool.tile([P, 2, P], F32, name="turned")
+        nc.tensor.transpose(gate_turned[:, 0, :], gate_rows[:], ident[:])
+        nc.scalar.copy(gate_cols[:], gate_turned[:, 0, 0 : S // P])
+
+        pairs = keep.tile([P, 2, S + P], F32, name="pairs")
+        rounded_slots = []
+        window = [keep.tile([P, D * T], F32, name="window%d" % u) for u in range(2)]
+        wm_grouped = [keep.tile([P, 4, P, 4], BF16, name="wm_grouped%d" % o, align_bytes=64) for o in range(D)]
+        wm_codes = [keep.tile([P, N], U32, name="wm_codes%d" % o, align_bytes=64) for o in range(D)]
+        wm_scales = [keep.tile([P, N], U8, name="wm_scales%d" % o, align_bytes=64) for o in range(D)]
+
+        def slot_tile(j):
+            e = j * P // C
+            acc = acc_pool.tile([P, H], F32, name="acc")
+            nc.tensor.matmul_mx(
+                out=acc[:],
+                lhsT=gathered[j][0].bitcast(X4),
+                lhsT_scale=gathered[j][1],
+                rhs=ww[e].bitcast(X4),
+                rhs_scale=ws[4 * e : P, :],
+                start=True,
+                stop=True,
+            )
+            y = ring.tile([P, 2, P, 2], F32, name="y")
+            nc.scalar.activation(y[:], acc[:].rearrange("s (p u d) -> s u p d", u=2, d=2), GELU)
+            c_slots = ring.tile([P, H], BF16, name="c_slots")
+            nc.scalar.activation(
+                c_slots[:], y[:].rearrange("s u p d -> s (u p d)"), COPY, scale=gate_cols[:, j : j + 1]
+            )
+            rounded_slots.append(c_slots[:].bitcast(F32))
+
+        def turn_and_scatter(step):
+            halves = [u for u in range(2) if 0 <= step - u < S // P]
+            cols = slice(step * P, (step + 1) * P)
+            turned = turn_pool.tile([P, 2, P], F32, name="turned")
+            for u in halves:
+                nc.tensor.transpose(turned[:, u, :], rounded_slots[step - u][:, u * P : (u + 1) * P], ident[:])
+            us = slice(halves[0], halves[-1] + 1)
+            nc.scalar.copy(pairs[:, us, cols], turned[:, us, :])
+            for u in halves:
+                listed = offsets[:, (step - u) * P // 16 : (step - u + 1) * P // 16]
+                nc.vector.tensor_copy(window[u][:].indirect(listed), pairs[:, u, cols])
+
+        def group_wm(o, half):
+            ms = slice(half * 64, (half + 1) * 64)
+            nc.gpsimd.tensor_scalar(
+                wm_grouped[o][:, :, ms, :].rearrange("p s m j -> p m s j"),
+                wm_raw[o][:].rearrange("p j (m s) -> p m s j", s=4)[:, ms, :, :],
+                1.0,
+                0.0,
+                MULT,
+                ADD,
+            )
+
+        def quantize_wm(o):
+            nc.vector.quantize_mx(
+                out=wm_codes[o][:].bitcast(X4),
+                scales=wm_scales[o][:],
+                in_=wm_grouped[o][:].rearrange("p s m j -> p (s m j)"),
+            )
+
+        for j in range(S // P):
+            slot_tile(j)
+            if j < 2:
+                gather(*GATHERS[j + 2])
+            if j == 1:
+                load_wm(0)
+                load_wm(1)
+            turn_and_scatter(j)
+        for o in range(D):
+            group_wm(o, 0)
+            group_wm(o, 1)
+            quantize_wm(o)
+        turn_and_scatter(S // P)
+
+        c_grouped = [keep.tile([P, D, TC, 2], F32, name="c_grouped%d" % k, align_bytes=64) for k in range(CHUNKS)]
+
+        def window_cols(u, k):
+            return window[u][:].rearrange("p (o t) -> p o t", o=D)[:, :, k * TC : (k + 1) * TC]
+
+        for k in range(CHUNKS):
+            nc.scalar.copy(c_grouped[k][:, :, :, 0], window_cols(0, k))
+
+        c_codes = [keep.tile([P, D * TC], U32, name="c_codes%d" % k, align_bytes=64) for k in range(CHUNKS)]
+        c_scales = [keep.tile([P, D * TC], U8, name="c_scales%d" % k, align_bytes=64) for k in range(CHUNKS)]
+        o_codes = keep.tile([P, T], U32, name="o_codes", align_bytes=64)
+        o_scales = keep.tile([P, T], U8, name="o_scales", align_bytes=64)
+        out_rows = out_0.rearrange("(p s) t -> p s t", s=4)
+        out_words = out_1[0].rearrange("p t d -> p (t d)").bitcast(I32)
+
+        for k in range(CHUNKS):
+            move = nc.vector.tensor_copy if k < CHUNKS - 1 else nc.scalar.copy
+            move(c_grouped[k][:, :, :, 1], window_cols(1, k))
+            nc.vector.quantize_mx(
+                out=c_codes[k][:].bitcast(X4),
+                scales=c_scales[k][:],
+                in_=c_grouped[k][:].rearrange("p o t u -> p (o t u)").bitcast(BF16),
+            )
+        for k in range(CHUNKS):
+            cols = slice(k * TC, (k + 1) * TC)
+            acc = acc_pool.tile([P, 4, TC], F32, name="acc")
+            for s in range(4):
+                for o in range(D):
+                    nc.tensor.matmul_mx(
+                        out=acc[:, s, :],
+                        lhsT=wm_codes[o][:, s * P : (s + 1) * P].bitcast(X4),
+                        lhsT_scale=wm_scales[o][:, s * P : (s + 1) * P],
+                        rhs=c_codes[k][:, o * TC : (o + 1) * TC].bitcast(X4),
+                        rhs_scale=c_scales[k][:, o * TC : (o + 1) * TC],
+                        start=(o == 0),
+                        stop=(o == D - 1),
+                    )
+            result = keep.tile([P, 4, TC], F32, name="result%d" % k)
+            nc.scalar.copy(result[:], acc[:])
+            nc.sync.dma_start(out_rows[:, :, cols], result[:])
+            rounded = keep.tile([P, TC, 4], BF16, name="rounded%d" % k, align_bytes=64)
+            nc.vector.tensor_copy(rounded[:], result[:].rearrange("p s t -> p t s"))
+            nc.vector.quantize_mx(
+                out=o_codes[:, cols].bitcast(X4),
+                scales=o_scales[:, cols],
+                in_=rounded[:].rearrange("p t s -> p (t s)"),
+            )
+            nc.sync.dma_start(out_words[:, cols], o_codes[:, cols].bitcast(I32))
+        for q in range(4):
+            queue = nc.sync if q % 2 == 0 else nc.scalar
+            queue.dma_start(
+                out_2[0, 4 * q : 4 * q + 4, :].bitcast(I32), o_scales[32 * q : 32 * q + 4, :].bitcast(I32)
+            )

@@ -16,9 +16,11 @@ U16 = mybir.dt.uint16
 U8 = mybir.dt.uint8
 X4 = mybir.dt.float8_e4m3fn_x4
 GELU = mybir.ActivationFunctionType.Gelu_apprx_tanh
-COPY = mybir.ActivationFunctionType.Copy
 
-GATHERS = ((0, 128), (128, 256), (256, 512), (512, 1024))
+FIRST = 256
+SCATTERS = ((0, 0, 128), (0, 128, 256), (1, 0, 256), (0, 256, 512), (1, 256, 512), (0, 512, 768),
+            (0, 768, 1024), (1, 512, 1024))
+WM_PIECES = 4
 MULT = mybir.AluOpType.mult
 ADD = mybir.AluOpType.add
 TC = 128
@@ -32,18 +34,16 @@ def tile_moe_mhm_gelu_kernel(
     with ExitStack() as ctx:
         keep = ctx.enter_context(tc.tile_pool(name="keep", bufs=1))
         ring = ctx.enter_context(tc.tile_pool(name="ring", bufs=3))
-        pair = ctx.enter_context(tc.tile_pool(name="pair", bufs=2))
         acc_pool = ctx.enter_context(tc.psum_pool(name="acc", bufs=4))
         turn_pool = ctx.enter_context(tc.psum_pool(name="turn", bufs=3))
 
         offsets = keep.tile([P, S // 16], U16, name="offsets")
-        xw = keep.tile([P, D * T], U32, name="xw", tag="then_wm1", align_bytes=64)
-        xs = keep.tile([P, D * T], U8, name="xs", align_bytes=64)
+        xw = keep.tile([P, D * T], U32, name="xw", align_bytes=64)
+        xs = keep.tile([P, D * T], U8, name="xs", tag="then_words", align_bytes=64)
         ws = keep.tile([P, H], U8, name="ws", align_bytes=64)
         w_first = keep.tile([P, H], U32, name="w_first", align_bytes=64)
         ww = [w_first[:]]
         gate_cols = keep.tile([P, S // P], F32, name="gate_cols")
-        wm_raw = []
         ident = keep.tile([P, P], F32, name="ident")
         warm_in = keep.tile([P, 1], F32, name="warm_in", tag="then_w", align_bytes=64)
         warm_out = keep.tile([P, 1], F32, name="warm_out", tag="then_wm0", align_bytes=64)
@@ -67,10 +67,6 @@ def tile_moe_mhm_gelu_kernel(
         def load_w(e):
             nc.sync.dma_start(ww[e].bitcast(I32), w_words[e, 0].rearrange("p l d -> p (l d)").bitcast(I32))
 
-        def load_wm(o):
-            wm_raw.append(keep.tile([P, 4, N], F32, name="wm_raw%d" % o, tag="then_wm%d" % o, align_bytes=64))
-            nc.sync.dma_start(wm_raw[o][:], wm[o * H : (o + 1) * H, :].rearrange("(p j) n -> p j n", j=4))
-
         load_w(0)
         for q in range(4):
             (nc.sync if q < 3 else nc.gpsimd).dma_start(
@@ -86,26 +82,28 @@ def tile_moe_mhm_gelu_kernel(
             ww.append(w_rest[:, (e - 1) * H : e * H])
             load_w(e)
 
-        gathered = {}
+        sg = keep.tile([P, S], U8, name="sg", align_bytes=64)
+        xg_first = keep.tile([P, FIRST], U32, name="xg_first", align_bytes=64)
+        nc.vector.tensor_copy(xg_first[:], xw[:].indirect(offsets[:, : FIRST // 16]))
+        nc.vector.tensor_copy(sg[:, :FIRST], xs[:].indirect(offsets[:, : FIRST // 16]))
+        nc.vector.tensor_copy(sg[:, FIRST:], xs[:].indirect(offsets[:, FIRST // 16 :]))
+        xg_rest = keep.tile([P, S - FIRST], U32, name="xg_rest", tag="then_words", align_bytes=64)
+        nc.vector.tensor_copy(xg_rest[:], xw[:].indirect(offsets[:, FIRST // 16 :]))
 
-        def gather(a, b):
-            xg = pair.tile([P, b - a], U32, name="xg", align_bytes=64)
-            sg = pair.tile([P, b - a], U8, name="sg", align_bytes=64)
-            nc.vector.tensor_copy(xg[:], xw[:].indirect(offsets[:, a // 16 : b // 16]))
-            nc.vector.tensor_copy(sg[:], xs[:].indirect(offsets[:, a // 16 : b // 16]))
-            for first in range(a, b, P):
-                part = slice(first - a, first - a + P)
-                gathered.setdefault(first // P, (xg[:, part], sg[:, part]))
-
-        for a, b in GATHERS[:2]:
-            gather(a, b)
+        def gathered_words(j):
+            if j * P < FIRST:
+                return xg_first[:, j * P : (j + 1) * P]
+            return xg_rest[:, j * P - FIRST : (j + 1) * P - FIRST]
 
         gate_turned = turn_pool.tile([P, 2, P], F32, name="turned")
         nc.tensor.transpose(gate_turned[:, 0, :], gate_rows[:], ident[:])
         nc.scalar.copy(gate_cols[:], gate_turned[:, 0, 0 : S // P])
 
-        pairs = keep.tile([P, 2, S + P], F32, name="pairs")
-        rounded_slots = []
+        wm_raw = keep.tile([P, D, 4, N], F32, name="wm_raw", tag="then_wm0", align_bytes=64)
+        for o in range(D):
+            nc.sync.dma_start(wm_raw[:, o], wm[o * H : (o + 1) * H, :].rearrange("(p j) n -> p j n", j=4))
+
+        pairs = keep.tile([P, 2, S], F32, name="pairs")
         window = [keep.tile([P, D * T], F32, name="window%d" % u) for u in range(2)]
         wm_grouped = [keep.tile([P, 4, P, 4], BF16, name="wm_grouped%d" % o, align_bytes=64) for o in range(D)]
         wm_codes = [keep.tile([P, N], U32, name="wm_codes%d" % o, align_bytes=64) for o in range(D)]
@@ -113,11 +111,12 @@ def tile_moe_mhm_gelu_kernel(
 
         def slot_tile(j):
             e = j * P // C
+            cols = slice(j * P, (j + 1) * P)
             acc = acc_pool.tile([P, H], F32, name="acc")
             nc.tensor.matmul_mx(
                 out=acc[:],
-                lhsT=gathered[j][0].bitcast(X4),
-                lhsT_scale=gathered[j][1],
+                lhsT=gathered_words(j).bitcast(X4),
+                lhsT_scale=sg[:, cols],
                 rhs=ww[e].bitcast(X4),
                 rhs_scale=ws[4 * e : P, :],
                 start=True,
@@ -126,33 +125,26 @@ def tile_moe_mhm_gelu_kernel(
             y = ring.tile([P, 2, P, 2], F32, name="y")
             nc.scalar.activation(y[:], acc[:].rearrange("s (p u d) -> s u p d", u=2, d=2), GELU)
             c_slots = ring.tile([P, H], BF16, name="c_slots")
-            nc.scalar.activation(
-                c_slots[:], y[:].rearrange("s u p d -> s (u p d)"), COPY, scale=gate_cols[:, j : j + 1]
-            )
-            rounded_slots.append(c_slots[:].bitcast(F32))
-
-        def turn_and_scatter(step):
-            halves = [u for u in range(2) if 0 <= step - u < S // P]
-            cols = slice(step * P, (step + 1) * P)
-            turned = turn_pool.tile([P, 2, P], F32, name="turned")
-            for u in halves:
-                nc.tensor.transpose(turned[:, u, :], rounded_slots[step - u][:, u * P : (u + 1) * P], ident[:])
-            us = slice(halves[0], halves[-1] + 1)
-            nc.scalar.copy(pairs[:, us, cols], turned[:, us, :])
-            for u in halves:
-                listed = offsets[:, (step - u) * P // 16 : (step - u + 1) * P // 16]
-                nc.vector.tensor_copy(window[u][:].indirect(listed), pairs[:, u, cols])
-
-        def group_wm(o, half):
-            ms = slice(half * 64, (half + 1) * 64)
             nc.gpsimd.tensor_scalar(
-                wm_grouped[o][:, :, ms, :].rearrange("p s m j -> p m s j"),
-                wm_raw[o][:].rearrange("p j (m s) -> p m s j", s=4)[:, ms, :, :],
-                1.0,
-                0.0,
-                MULT,
-                ADD,
+                c_slots[:], y[:].rearrange("s u p d -> s (u p d)"), gate_cols[:, j : j + 1], 0.0, MULT, ADD
             )
+            words = c_slots[:].bitcast(F32)
+            turned = turn_pool.tile([P, 2, P], F32, name="turned")
+            for u in range(2):
+                nc.tensor.transpose(turned[:, u, :], words[:, u * P : (u + 1) * P], ident[:])
+            nc.scalar.copy(pairs[:, :, cols], turned[:])
+
+        def scatter(u, a, b):
+            nc.vector.tensor_copy(window[u][:].indirect(offsets[:, a // 16 : b // 16]), pairs[:, u, a:b])
+
+        def group_wm(o, piece):
+            ms = slice(piece * P // WM_PIECES, (piece + 1) * P // WM_PIECES)
+            dst = wm_grouped[o][:, :, ms, :].rearrange("p s m j -> p m s j")
+            src = wm_raw[:, o].rearrange("p j (m s) -> p m s j", s=4)[:, ms, :, :]
+            if o == D - 1:
+                nc.scalar.copy(dst, src)
+            else:
+                nc.gpsimd.tensor_scalar(dst, src, 1.0, 0.0, MULT, ADD)
 
         def quantize_wm(o):
             nc.vector.quantize_mx(
@@ -163,17 +155,14 @@ def tile_moe_mhm_gelu_kernel(
 
         for j in range(S // P):
             slot_tile(j)
-            if j < 2:
-                gather(*GATHERS[j + 2])
-            if j == 1:
-                load_wm(0)
-                load_wm(1)
-            turn_and_scatter(j)
+            for u, a, b in SCATTERS[:-1]:
+                if b == (j + 1) * P:
+                    scatter(u, a, b)
         for o in range(D):
-            group_wm(o, 0)
-            group_wm(o, 1)
+            for piece in range(WM_PIECES):
+                group_wm(o, piece)
             quantize_wm(o)
-        turn_and_scatter(S // P)
+        scatter(*SCATTERS[-1])
 
         c_grouped = [keep.tile([P, D, TC, 2], F32, name="c_grouped%d" % k, align_bytes=64) for k in range(CHUNKS)]
 
@@ -191,7 +180,7 @@ def tile_moe_mhm_gelu_kernel(
         out_words = out_1[0].rearrange("p t d -> p (t d)").bitcast(I32)
 
         for k in range(CHUNKS):
-            move = nc.vector.tensor_copy if k < CHUNKS - 1 else nc.scalar.copy
+            move = nc.vector.tensor_copy if k == 0 else nc.scalar.copy
             move(c_grouped[k][:, :, :, 1], window_cols(1, k))
             nc.vector.quantize_mx(
                 out=c_codes[k][:].bitcast(X4),
@@ -222,7 +211,9 @@ def tile_moe_mhm_gelu_kernel(
                 scales=o_scales[:, cols],
                 in_=rounded[:].rearrange("p t s -> p (t s)"),
             )
-            nc.sync.dma_start(out_words[:, cols], o_codes[:, cols].bitcast(I32))
+            if k >= CHUNKS - 2:
+                done = slice(0, (k + 1) * TC) if k == CHUNKS - 2 else cols
+                nc.sync.dma_start(out_words[:, done], o_codes[:, done].bitcast(I32))
         for q in range(4):
             queue = nc.sync if q % 2 == 0 else nc.scalar
             queue.dma_start(

@@ -17,10 +17,14 @@ U8 = mybir.dt.uint8
 X4 = mybir.dt.float8_e4m3fn_x4
 GELU = mybir.ActivationFunctionType.Gelu_apprx_tanh
 
+HALF = S // 2
 FIRST = 256
-SCATTERS = ((0, 0, 128), (0, 128, 256), (1, 0, 256), (0, 256, 512), (1, 256, 512), (0, 512, 768),
-            (0, 768, 1024), (1, 512, 1024))
+SCATTERS = (
+    (0, 0, 128), (1, 0, 128), (0, 128, 256), (1, 128, 256), (0, 256, 512), (1, 256, 512), (0, 512, 768),
+    (0, 768, 1024), (1, 512, 896), (1, 896, 1024),
+)
 WM_PIECES = 4
+COPY = mybir.ActivationFunctionType.Copy
 MULT = mybir.AluOpType.mult
 ADD = mybir.AluOpType.add
 TC = 128
@@ -34,7 +38,7 @@ def tile_moe_mhm_gelu_kernel(
     with ExitStack() as ctx:
         keep = ctx.enter_context(tc.tile_pool(name="keep", bufs=1))
         ring = ctx.enter_context(tc.tile_pool(name="ring", bufs=3))
-        acc_pool = ctx.enter_context(tc.psum_pool(name="acc", bufs=4))
+        acc_pool = ctx.enter_context(tc.psum_pool(name="acc", bufs=2))
         turn_pool = ctx.enter_context(tc.psum_pool(name="turn", bufs=3))
 
         offsets = keep.tile([P, S // 16], U16, name="offsets")
@@ -46,12 +50,14 @@ def tile_moe_mhm_gelu_kernel(
         gate_cols = keep.tile([P, S // P], F32, name="gate_cols")
         ident = keep.tile([P, P], F32, name="ident")
         warm_in = keep.tile([P, 1], F32, name="warm_in", tag="then_w", align_bytes=64)
-        warm_out = keep.tile([P, 1], F32, name="warm_out", tag="then_wm0", align_bytes=64)
+        warm_bias = keep.tile([P, 1], F32, name="warm_bias", tag="then_wm0", align_bytes=64)
+        zero = keep.tile([P, 1], F32, name="zero")
+        gate_rows = keep.tile([P, P], F32, name="gate_rows")
 
         nc.gpsimd.memset(xs[:].bitcast(I32), 0)
         nc.gpsimd.memset(ws[:].bitcast(I32), 0)
         nc.vector.memset(warm_in[:], 0.0)
-        nc.scalar.activation(warm_out[:], warm_in[:], GELU)
+        nc.vector.memset(warm_bias[:], 0.0)
 
         nc.sync.dma_start(offsets[:], offs)
         nc.sync.dma_start(
@@ -59,23 +65,23 @@ def tile_moe_mhm_gelu_kernel(
             x_words.rearrange("o p t d -> p o (t d)").bitcast(I32),
         )
         for q in range(4):
-            nc.sync.dma_start(
+            nc.scalar.dma_start(
                 xs[32 * q : 32 * q + 4, :].bitcast(I32).rearrange("r (o t) -> r o t", o=D),
                 x_scales[:, 4 * q : 4 * q + 4, :].rearrange("o r t -> r o t").bitcast(I32),
             )
+        nc.scalar.activation(zero[:], warm_in[:], GELU, bias=warm_bias[:])
 
         def load_w(e):
             nc.sync.dma_start(ww[e].bitcast(I32), w_words[e, 0].rearrange("p l d -> p (l d)").bitcast(I32))
 
         load_w(0)
         for q in range(4):
-            (nc.sync if q < 3 else nc.gpsimd).dma_start(
+            nc.sync.dma_start(
                 ws[32 * q : 32 * q + 16, :].bitcast(I32),
                 w_scales[:, 0, 4 * q : 4 * q + 4, :].bitcast(I32),
             )
 
         make_identity(nc, ident[:])
-        gate_rows = keep.tile([P, P], F32, name="gate_rows", tag="then_wm0", align_bytes=64)
         nc.sync.dma_start(gate_rows[:], gate[0:16, :].rearrange("a (j c) -> (a j) c", c=P))
         w_rest = keep.tile([P, (E - 1) * H], U32, name="w_rest", tag="then_w", align_bytes=64)
         for e in range(1, E):
@@ -83,17 +89,15 @@ def tile_moe_mhm_gelu_kernel(
             load_w(e)
 
         sg = keep.tile([P, S], U8, name="sg", align_bytes=64)
-        xg_first = keep.tile([P, FIRST], U32, name="xg_first", align_bytes=64)
-        nc.vector.tensor_copy(xg_first[:], xw[:].indirect(offsets[:, : FIRST // 16]))
+        xg_first = keep.tile([P, HALF], U32, name="xg_first", align_bytes=64)
+        nc.vector.tensor_copy(xg_first[:], xw[:].indirect(offsets[:, : HALF // 16]))
         nc.vector.tensor_copy(sg[:, :FIRST], xs[:].indirect(offsets[:, : FIRST // 16]))
         nc.vector.tensor_copy(sg[:, FIRST:], xs[:].indirect(offsets[:, FIRST // 16 :]))
-        xg_rest = keep.tile([P, S - FIRST], U32, name="xg_rest", tag="then_words", align_bytes=64)
-        nc.vector.tensor_copy(xg_rest[:], xw[:].indirect(offsets[:, FIRST // 16 :]))
+        xg_rest = keep.tile([P, HALF], U32, name="xg_rest", tag="then_words", align_bytes=64)
+        nc.vector.tensor_copy(xg_rest[:], xw[:].indirect(offsets[:, HALF // 16 :]))
 
         def gathered_words(j):
-            if j * P < FIRST:
-                return xg_first[:, j * P : (j + 1) * P]
-            return xg_rest[:, j * P - FIRST : (j + 1) * P - FIRST]
+            return (xg_first, xg_rest)[j * P // HALF][:, j * P % HALF : j * P % HALF + P]
 
         gate_turned = turn_pool.tile([P, 2, P], F32, name="turned")
         nc.tensor.transpose(gate_turned[:, 0, :], gate_rows[:], ident[:])
@@ -104,10 +108,13 @@ def tile_moe_mhm_gelu_kernel(
             nc.sync.dma_start(wm_raw[:, o], wm[o * H : (o + 1) * H, :].rearrange("(p j) n -> p j n", j=4))
 
         pairs = keep.tile([P, 2, S], F32, name="pairs")
+        last_first = keep.tile([P, C], F32, name="last_first", tag="then_codes", align_bytes=64)
         window = [keep.tile([P, D * T], F32, name="window%d" % u) for u in range(2)]
         wm_grouped = [keep.tile([P, 4, P, 4], BF16, name="wm_grouped%d" % o, align_bytes=64) for o in range(D)]
-        wm_codes = [keep.tile([P, N], U32, name="wm_codes%d" % o, align_bytes=64) for o in range(D)]
+        wm_codes = []
         wm_scales = [keep.tile([P, N], U8, name="wm_scales%d" % o, align_bytes=64) for o in range(D)]
+
+        words = []
 
         def slot_tile(j):
             e = j * P // C
@@ -123,19 +130,33 @@ def tile_moe_mhm_gelu_kernel(
                 stop=True,
             )
             y = ring.tile([P, 2, P, 2], F32, name="y")
-            nc.scalar.activation(y[:], acc[:].rearrange("s (p u d) -> s u p d", u=2, d=2), GELU)
+            nc.scalar.activation(y[:], acc[:].rearrange("s (p u d) -> s u p d", u=2, d=2), GELU, bias=zero[:])
             c_slots = ring.tile([P, H], BF16, name="c_slots")
-            nc.gpsimd.tensor_scalar(
-                c_slots[:], y[:].rearrange("s u p d -> s (u p d)"), gate_cols[:, j : j + 1], 0.0, MULT, ADD
-            )
-            words = c_slots[:].bitcast(F32)
-            turned = turn_pool.tile([P, 2, P], F32, name="turned")
-            for u in range(2):
-                nc.tensor.transpose(turned[:, u, :], words[:, u * P : (u + 1) * P], ident[:])
-            nc.scalar.copy(pairs[:, :, cols], turned[:])
+            flat = y[:].rearrange("s u p d -> s (u p d)")
+            if j == 0:
+                nc.scalar.activation(c_slots[:], flat, COPY, scale=gate_cols[:, j : j + 1])
+            else:
+                nc.gpsimd.tensor_scalar(c_slots[:], flat, gate_cols[:, j : j + 1], 0.0, MULT, ADD)
+            words.append(c_slots[:].bitcast(F32))
+            if e < E - 1:
+                turned = turn_pool.tile([P, 2, P], F32, name="turned")
+                for u in range(2):
+                    nc.tensor.transpose(turned[:, u, :], words[j][:, u * P : (u + 1) * P], ident[:])
+                move = nc.vector.tensor_copy if j == 0 else nc.scalar.copy
+                move(pairs[:, :, cols], turned[:])
+                return
+            turned = turn_pool.tile([P, 3, P], F32, name="turned")
+            nc.tensor.transpose(turned[:, 0, :], words[j][:, :P], ident[:])
+            if j == S // P - 1:
+                for i in range(2):
+                    nc.tensor.transpose(turned[:, 1 + i, :], words[j - 1 + i][:, P:], ident[:])
+            nc.scalar.copy(last_first[:, j * P % C : j * P % C + P], turned[:, 0, :])
+            if j == S // P - 1:
+                nc.scalar.copy(pairs[:, 1, S - C :], turned[:, 1:, :].rearrange("p i s -> p (i s)"))
 
         def scatter(u, a, b):
-            nc.vector.tensor_copy(window[u][:].indirect(offsets[:, a // 16 : b // 16]), pairs[:, u, a:b])
+            src = last_first[:] if (u, a) == (0, S - C) else pairs[:, u, a:b]
+            nc.vector.tensor_copy(window[u][:].indirect(offsets[:, a // 16 : b // 16]), src)
 
         def group_wm(o, piece):
             ms = slice(piece * P // WM_PIECES, (piece + 1) * P // WM_PIECES)
@@ -147,6 +168,8 @@ def tile_moe_mhm_gelu_kernel(
                 nc.gpsimd.tensor_scalar(dst, src, 1.0, 0.0, MULT, ADD)
 
         def quantize_wm(o):
+            tag = ("wm_codes0", "then_codes")[o]
+            wm_codes.append(keep.tile([P, N], U32, name="wm_codes%d" % o, tag=tag, align_bytes=64))
             nc.vector.quantize_mx(
                 out=wm_codes[o][:].bitcast(X4),
                 scales=wm_scales[o][:],
@@ -155,14 +178,26 @@ def tile_moe_mhm_gelu_kernel(
 
         for j in range(S // P):
             slot_tile(j)
-            for u, a, b in SCATTERS[:-1]:
+            for u, a, b in SCATTERS[:-2]:
                 if b == (j + 1) * P:
                     scatter(u, a, b)
+        scatter(*SCATTERS[-2])
         for o in range(D):
             for piece in range(WM_PIECES):
                 group_wm(o, piece)
             quantize_wm(o)
         scatter(*SCATTERS[-1])
+        spare = turn_pool.tile([P, N], F32, name="spare", tag="spare", bufs=1)
+        for r in range(3):
+            nc.tensor.matmul_mx(
+                out=spare[:],
+                lhsT=wm_codes[1][:, 0:P].bitcast(X4),
+                lhsT_scale=wm_scales[1][:, 0:P],
+                rhs=wm_codes[1][:].bitcast(X4),
+                rhs_scale=wm_scales[1][:],
+                start=True,
+                stop=True,
+            )
 
         c_grouped = [keep.tile([P, D, TC, 2], F32, name="c_grouped%d" % k, align_bytes=64) for k in range(CHUNKS)]
 
@@ -189,7 +224,7 @@ def tile_moe_mhm_gelu_kernel(
             )
         for k in range(CHUNKS):
             cols = slice(k * TC, (k + 1) * TC)
-            acc = acc_pool.tile([P, 4, TC], F32, name="acc")
+            acc = acc_pool.tile([P, 4, TC], F32, name="acc", tag=("merged", "acc")[k // 2])
             for s in range(4):
                 for o in range(D):
                     nc.tensor.matmul_mx(

@@ -5,7 +5,10 @@ from concourse.masks import make_identity
 
 D, T, E, C, H, N = 2, 512, 4, 256, 512, 512
 P = 128
+PACK = 4
+QUADS = 4
 S = E * C
+TILES = S // P
 FLOPS = 2 * H * H * S + 2 * D * H * N * T
 
 F32 = mybir.dt.float32
@@ -16,19 +19,15 @@ U16 = mybir.dt.uint16
 U8 = mybir.dt.uint8
 X4 = mybir.dt.float8_e4m3fn_x4
 GELU = mybir.ActivationFunctionType.Gelu_apprx_tanh
-
-HALF = S // 2
-FIRST = 256
-SCATTERS = (
-    (0, 0, 128), (1, 0, 128), (0, 128, 256), (1, 128, 256), (0, 256, 512), (1, 256, 512), (0, 512, 768),
-    (0, 768, 1024), (1, 512, 896), (1, 896, 1024),
-)
-WM_PIECES = 4
 COPY = mybir.ActivationFunctionType.Copy
 MULT = mybir.AluOpType.mult
 ADD = mybir.AluOpType.add
+
+HALF = S // 2
+WM_PIECES = 4
 TC = 128
 CHUNKS = T // TC
+WARM_PASSES = 3
 
 
 def tile_moe_mhm_gelu_kernel(
@@ -47,42 +46,42 @@ def tile_moe_mhm_gelu_kernel(
         ws = keep.tile([P, H], U8, name="ws", align_bytes=64)
         w_first = keep.tile([P, H], U32, name="w_first", align_bytes=64)
         ww = [w_first[:]]
-        gate_cols = keep.tile([P, S // P], F32, name="gate_cols")
+        gate_cols = keep.tile([P, TILES], F32, name="gate_cols")
         ident = keep.tile([P, P], F32, name="ident")
-        warm_in = keep.tile([P, 1], F32, name="warm_in", tag="then_w", align_bytes=64)
-        warm_bias = keep.tile([P, 1], F32, name="warm_bias", tag="then_wm0", align_bytes=64)
+        zero_in = keep.tile([P, 1], F32, name="zero_in", tag="then_w", align_bytes=64)
+        zero_bias = keep.tile([P, 1], F32, name="zero_bias", tag="then_wm", align_bytes=64)
         zero = keep.tile([P, 1], F32, name="zero")
         gate_rows = keep.tile([P, P], F32, name="gate_rows")
 
         nc.gpsimd.memset(xs[:].bitcast(I32), 0)
         nc.gpsimd.memset(ws[:].bitcast(I32), 0)
-        nc.vector.memset(warm_in[:], 0.0)
-        nc.vector.memset(warm_bias[:], 0.0)
+        nc.vector.memset(zero_in[:], 0.0)
+        nc.vector.memset(zero_bias[:], 0.0)
 
         nc.sync.dma_start(offsets[:], offs)
         nc.sync.dma_start(
             xw[:].bitcast(I32).rearrange("p (o t) -> p o t", o=D),
             x_words.rearrange("o p t d -> p o (t d)").bitcast(I32),
         )
-        for q in range(4):
-            nc.scalar.dma_start(
+        for q in range(QUADS):
+            nc.sync.dma_start(
                 xs[32 * q : 32 * q + 4, :].bitcast(I32).rearrange("r (o t) -> r o t", o=D),
                 x_scales[:, 4 * q : 4 * q + 4, :].rearrange("o r t -> r o t").bitcast(I32),
             )
-        nc.scalar.activation(zero[:], warm_in[:], GELU, bias=warm_bias[:])
+        nc.scalar.activation(zero[:], zero_in[:], GELU, bias=zero_bias[:])
 
         def load_w(e):
             nc.sync.dma_start(ww[e].bitcast(I32), w_words[e, 0].rearrange("p l d -> p (l d)").bitcast(I32))
 
         load_w(0)
-        for q in range(4):
+        for q in range(QUADS):
             nc.sync.dma_start(
-                ws[32 * q : 32 * q + 16, :].bitcast(I32),
+                ws[32 * q : 32 * q + 4 * E, :].bitcast(I32),
                 w_scales[:, 0, 4 * q : 4 * q + 4, :].bitcast(I32),
             )
 
         make_identity(nc, ident[:])
-        nc.sync.dma_start(gate_rows[:], gate[0:16, :].rearrange("a (j c) -> (a j) c", c=P))
+        nc.sync.dma_start(gate_rows[:], gate[0 : P // TILES, :].rearrange("a (j c) -> (a j) c", c=P))
         w_rest = keep.tile([P, (E - 1) * H], U32, name="w_rest", tag="then_w", align_bytes=64)
         for e in range(1, E):
             ww.append(w_rest[:, (e - 1) * H : e * H])
@@ -91,8 +90,8 @@ def tile_moe_mhm_gelu_kernel(
         sg = keep.tile([P, S], U8, name="sg", align_bytes=64)
         xg_first = keep.tile([P, HALF], U32, name="xg_first", align_bytes=64)
         nc.vector.tensor_copy(xg_first[:], xw[:].indirect(offsets[:, : HALF // 16]))
-        nc.vector.tensor_copy(sg[:, :FIRST], xs[:].indirect(offsets[:, : FIRST // 16]))
-        nc.vector.tensor_copy(sg[:, FIRST:], xs[:].indirect(offsets[:, FIRST // 16 :]))
+        nc.vector.tensor_copy(sg[:, :C], xs[:].indirect(offsets[:, : C // 16]))
+        nc.vector.tensor_copy(sg[:, C:], xs[:].indirect(offsets[:, C // 16 :]))
         xg_rest = keep.tile([P, HALF], U32, name="xg_rest", tag="then_words", align_bytes=64)
         nc.vector.tensor_copy(xg_rest[:], xw[:].indirect(offsets[:, HALF // 16 :]))
 
@@ -101,20 +100,19 @@ def tile_moe_mhm_gelu_kernel(
 
         gate_turned = turn_pool.tile([P, 2, P], F32, name="turned")
         nc.tensor.transpose(gate_turned[:, 0, :], gate_rows[:], ident[:])
-        nc.scalar.copy(gate_cols[:], gate_turned[:, 0, 0 : S // P])
+        nc.scalar.copy(gate_cols[:], gate_turned[:, 0, 0:TILES])
 
-        wm_raw = keep.tile([P, D, 4, N], F32, name="wm_raw", tag="then_wm0", align_bytes=64)
+        wm_raw = keep.tile([P, D, PACK, N], F32, name="wm_raw", tag="then_wm", align_bytes=64)
         for o in range(D):
-            nc.sync.dma_start(wm_raw[:, o], wm[o * H : (o + 1) * H, :].rearrange("(p j) n -> p j n", j=4))
+            nc.sync.dma_start(wm_raw[:, o], wm[o * H : (o + 1) * H, :].rearrange("(p d) n -> p d n", d=PACK))
 
         pairs = keep.tile([P, 2, S], F32, name="pairs")
-        last_first = keep.tile([P, C], F32, name="last_first", tag="then_codes", align_bytes=64)
+        last_pairs0 = keep.tile([P, C], F32, name="last_pairs0", tag="then_codes", align_bytes=64)
         window = [keep.tile([P, D * T], F32, name="window%d" % u) for u in range(2)]
-        wm_grouped = [keep.tile([P, 4, P, 4], BF16, name="wm_grouped%d" % o, align_bytes=64) for o in range(D)]
+        wm_grouped = [keep.tile([P, PACK, P, PACK], BF16, name="wm_grouped%d" % o, align_bytes=64) for o in range(D)]
         wm_codes = []
         wm_scales = [keep.tile([P, N], U8, name="wm_scales%d" % o, align_bytes=64) for o in range(D)]
-
-        words = []
+        slot_pairs = []
 
         def slot_tile(j):
             e = j * P // C
@@ -130,38 +128,38 @@ def tile_moe_mhm_gelu_kernel(
                 stop=True,
             )
             y = ring.tile([P, 2, P, 2], F32, name="y")
-            nc.scalar.activation(y[:], acc[:].rearrange("s (p u d) -> s u p d", u=2, d=2), GELU, bias=zero[:])
+            nc.scalar.activation(y[:], acc[:].rearrange("s (p u i) -> s u p i", u=2, i=2), GELU, bias=zero[:])
             c_slots = ring.tile([P, H], BF16, name="c_slots")
-            flat = y[:].rearrange("s u p d -> s (u p d)")
+            y_flat = y[:].rearrange("s u p i -> s (u p i)")
             if j == 0:
-                nc.scalar.activation(c_slots[:], flat, COPY, scale=gate_cols[:, j : j + 1])
+                nc.scalar.activation(c_slots[:], y_flat, COPY, scale=gate_cols[:, j : j + 1])
             else:
-                nc.gpsimd.tensor_scalar(c_slots[:], flat, gate_cols[:, j : j + 1], 0.0, MULT, ADD)
-            words.append(c_slots[:].bitcast(F32))
+                nc.gpsimd.tensor_scalar(c_slots[:], y_flat, gate_cols[:, j : j + 1], 0.0, MULT, ADD)
+            slot_pairs.append(c_slots[:].bitcast(F32))
             if e < E - 1:
                 turned = turn_pool.tile([P, 2, P], F32, name="turned")
                 for u in range(2):
-                    nc.tensor.transpose(turned[:, u, :], words[j][:, u * P : (u + 1) * P], ident[:])
+                    nc.tensor.transpose(turned[:, u, :], slot_pairs[j][:, u * P : (u + 1) * P], ident[:])
                 move = nc.vector.tensor_copy if j == 0 else nc.scalar.copy
                 move(pairs[:, :, cols], turned[:])
                 return
-            turned = turn_pool.tile([P, 3, P], F32, name="turned")
-            nc.tensor.transpose(turned[:, 0, :], words[j][:, :P], ident[:])
-            if j == S // P - 1:
-                for i in range(2):
-                    nc.tensor.transpose(turned[:, 1 + i, :], words[j - 1 + i][:, P:], ident[:])
-            nc.scalar.copy(last_first[:, j * P % C : j * P % C + P], turned[:, 0, :])
-            if j == S // P - 1:
+            turned = turn_pool.tile([P, 1 + C // P, P], F32, name="turned")
+            nc.tensor.transpose(turned[:, 0, :], slot_pairs[j][:, :P], ident[:])
+            if j == TILES - 1:
+                for i in range(C // P):
+                    nc.tensor.transpose(turned[:, 1 + i, :], slot_pairs[TILES - C // P + i][:, P:], ident[:])
+            nc.scalar.copy(last_pairs0[:, j * P % C : j * P % C + P], turned[:, 0, :])
+            if j == TILES - 1:
                 nc.scalar.copy(pairs[:, 1, S - C :], turned[:, 1:, :].rearrange("p i s -> p (i s)"))
 
         def scatter(u, a, b):
-            src = last_first[:] if (u, a) == (0, S - C) else pairs[:, u, a:b]
+            src = last_pairs0[:] if (u, a) == (0, S - C) else pairs[:, u, a:b]
             nc.vector.tensor_copy(window[u][:].indirect(offsets[:, a // 16 : b // 16]), src)
 
         def group_wm(o, piece):
             ms = slice(piece * P // WM_PIECES, (piece + 1) * P // WM_PIECES)
-            dst = wm_grouped[o][:, :, ms, :].rearrange("p s m j -> p m s j")
-            src = wm_raw[:, o].rearrange("p j (m s) -> p m s j", s=4)[:, ms, :, :]
+            dst = wm_grouped[o][:, :, ms, :].rearrange("p s m d -> p m s d")
+            src = wm_raw[:, o].rearrange("p d (m s) -> p m s d", s=PACK)[:, ms, :, :]
             if o == D - 1:
                 nc.scalar.copy(dst, src)
             else:
@@ -173,22 +171,29 @@ def tile_moe_mhm_gelu_kernel(
             nc.vector.quantize_mx(
                 out=wm_codes[o][:].bitcast(X4),
                 scales=wm_scales[o][:],
-                in_=wm_grouped[o][:].rearrange("p s m j -> p (s m j)"),
+                in_=wm_grouped[o][:].rearrange("p s m d -> p (s m d)"),
             )
 
-        for j in range(S // P):
+        for j in range(TILES):
             slot_tile(j)
-            for u, a, b in SCATTERS[:-2]:
-                if b == (j + 1) * P:
-                    scatter(u, a, b)
-        scatter(*SCATTERS[-2])
-        for o in range(D):
-            for piece in range(WM_PIECES):
-                group_wm(o, piece)
-            quantize_wm(o)
-        scatter(*SCATTERS[-1])
+            end = (j + 1) * P
+            if end <= C:
+                scatter(0, end - P, end)
+                scatter(1, end - P, end)
+            elif end % C == 0:
+                scatter(0, end - C, end)
+                if end <= HALF:
+                    scatter(1, end - C, end)
+            if end == S - C:
+                for o in range(D):
+                    for piece in range(WM_PIECES):
+                        group_wm(o, piece)
+                quantize_wm(0)
+        scatter(1, HALF, S - P)
+        quantize_wm(1)
+        scatter(1, S - P, S)
         spare = turn_pool.tile([P, N], F32, name="spare", tag="spare", bufs=1)
-        for r in range(3):
+        for warm_pass in range(WARM_PASSES):
             nc.tensor.matmul_mx(
                 out=spare[:],
                 lhsT=wm_codes[1][:, 0:P].bitcast(X4),
@@ -211,11 +216,11 @@ def tile_moe_mhm_gelu_kernel(
         c_scales = [keep.tile([P, D * TC], U8, name="c_scales%d" % k, align_bytes=64) for k in range(CHUNKS)]
         o_codes = keep.tile([P, T], U32, name="o_codes", align_bytes=64)
         o_scales = keep.tile([P, T], U8, name="o_scales", align_bytes=64)
-        out_rows = out_0.rearrange("(p s) t -> p s t", s=4)
+        out_rows = out_0.rearrange("(p s) t -> p s t", s=PACK)
         out_words = out_1[0].rearrange("p t d -> p (t d)").bitcast(I32)
 
         for k in range(CHUNKS):
-            move = nc.vector.tensor_copy if k == 0 else nc.scalar.copy
+            move = nc.vector.tensor_copy if k < CHUNKS // 2 else nc.scalar.copy
             move(c_grouped[k][:, :, :, 1], window_cols(1, k))
             nc.vector.quantize_mx(
                 out=c_codes[k][:].bitcast(X4),
@@ -224,11 +229,16 @@ def tile_moe_mhm_gelu_kernel(
             )
         for k in range(CHUNKS):
             cols = slice(k * TC, (k + 1) * TC)
-            acc = acc_pool.tile([P, 4, TC], F32, name="acc", tag=("merged", "acc")[k // 2])
-            for s in range(4):
+            merged = acc_pool.tile([P, PACK, TC], F32, name="merged", tag=("merged", "acc")[k // 2])
+            banks = [merged[:]]
+            if k == CHUNKS - 1:
+                second = turn_pool.tile([P, PACK // 2, TC], F32, name="turned")
+                banks = [merged[:, : PACK // 2, :], second[:]]
+            per_bank = PACK // len(banks)
+            for s in range(PACK):
                 for o in range(D):
                     nc.tensor.matmul_mx(
-                        out=acc[:, s, :],
+                        out=banks[s // per_bank][:, s % per_bank, :],
                         lhsT=wm_codes[o][:, s * P : (s + 1) * P].bitcast(X4),
                         lhsT_scale=wm_scales[o][:, s * P : (s + 1) * P],
                         rhs=c_codes[k][:, o * TC : (o + 1) * TC].bitcast(X4),
@@ -236,10 +246,11 @@ def tile_moe_mhm_gelu_kernel(
                         start=(o == 0),
                         stop=(o == D - 1),
                     )
-            result = keep.tile([P, 4, TC], F32, name="result%d" % k)
-            nc.scalar.copy(result[:], acc[:])
+            result = keep.tile([P, PACK, TC], F32, name="result%d" % k)
+            for i, bank in enumerate(banks):
+                nc.scalar.copy(result[:, i * per_bank : (i + 1) * per_bank, :], bank)
             nc.sync.dma_start(out_rows[:, :, cols], result[:])
-            rounded = keep.tile([P, TC, 4], BF16, name="rounded%d" % k, align_bytes=64)
+            rounded = keep.tile([P, TC, PACK], BF16, name="rounded%d" % k, align_bytes=64)
             nc.vector.tensor_copy(rounded[:], result[:].rearrange("p s t -> p t s"))
             nc.vector.quantize_mx(
                 out=o_codes[:, cols].bitcast(X4),
@@ -249,7 +260,7 @@ def tile_moe_mhm_gelu_kernel(
             if k >= CHUNKS - 2:
                 done = slice(0, (k + 1) * TC) if k == CHUNKS - 2 else cols
                 nc.sync.dma_start(out_words[:, done], o_codes[:, done].bitcast(I32))
-        for q in range(4):
+        for q in range(QUADS):
             queue = nc.sync if q % 2 == 0 else nc.scalar
             queue.dma_start(
                 out_2[0, 4 * q : 4 * q + 4, :].bitcast(I32), o_scales[32 * q : 32 * q + 4, :].bitcast(I32)

@@ -27,7 +27,6 @@ HALF = S // 2
 WM_PIECES = 4
 TC = 128
 CHUNKS = T // TC
-WARM_PASSES = 3
 
 
 def tile_moe_mhm_gelu_kernel(
@@ -107,12 +106,10 @@ def tile_moe_mhm_gelu_kernel(
             nc.sync.dma_start(wm_raw[:, o], wm[o * H : (o + 1) * H, :].rearrange("(p d) n -> p d n", d=PACK))
 
         pairs = keep.tile([P, 2, S], F32, name="pairs")
-        last_pairs0 = keep.tile([P, C], F32, name="last_pairs0", tag="then_codes", align_bytes=64)
         window = [keep.tile([P, D * T], F32, name="window%d" % u) for u in range(2)]
         wm_grouped = [keep.tile([P, PACK, P, PACK], BF16, name="wm_grouped%d" % o, align_bytes=64) for o in range(D)]
-        wm_codes = []
+        wm_codes = [keep.tile([P, N], U32, name="wm_codes%d" % o, align_bytes=64) for o in range(D)]
         wm_scales = [keep.tile([P, N], U8, name="wm_scales%d" % o, align_bytes=64) for o in range(D)]
-        slot_pairs = []
 
         def slot_tile(j):
             e = j * P // C
@@ -135,39 +132,26 @@ def tile_moe_mhm_gelu_kernel(
                 nc.scalar.activation(c_slots[:], y_flat, COPY, scale=gate_cols[:, j : j + 1])
             else:
                 nc.gpsimd.tensor_scalar(c_slots[:], y_flat, gate_cols[:, j : j + 1], 0.0, MULT, ADD)
-            slot_pairs.append(c_slots[:].bitcast(F32))
-            if e < E - 1:
-                turned = turn_pool.tile([P, 2, P], F32, name="turned")
-                for u in range(2):
-                    nc.tensor.transpose(turned[:, u, :], slot_pairs[j][:, u * P : (u + 1) * P], ident[:])
-                move = nc.vector.tensor_copy if j == 0 else nc.scalar.copy
-                move(pairs[:, :, cols], turned[:])
-                return
-            turned = turn_pool.tile([P, 1 + C // P, P], F32, name="turned")
-            nc.tensor.transpose(turned[:, 0, :], slot_pairs[j][:, :P], ident[:])
-            if j == TILES - 1:
-                for i in range(C // P):
-                    nc.tensor.transpose(turned[:, 1 + i, :], slot_pairs[TILES - C // P + i][:, P:], ident[:])
-            nc.scalar.copy(last_pairs0[:, j * P % C : j * P % C + P], turned[:, 0, :])
-            if j == TILES - 1:
-                nc.scalar.copy(pairs[:, 1, S - C :], turned[:, 1:, :].rearrange("p i s -> p (i s)"))
+            slot_pairs = c_slots[:].bitcast(F32)
+            turned = turn_pool.tile([P, 2, P], F32, name="turned")
+            for u in range(2):
+                nc.tensor.transpose(turned[:, u, :], slot_pairs[:, u * P : (u + 1) * P], ident[:])
+            move = nc.vector.tensor_copy if j == 0 else nc.scalar.copy
+            move(pairs[:, :, cols], turned[:])
 
         def scatter(u, a, b):
-            src = last_pairs0[:] if (u, a) == (0, S - C) else pairs[:, u, a:b]
-            nc.vector.tensor_copy(window[u][:].indirect(offsets[:, a // 16 : b // 16]), src)
+            nc.vector.tensor_copy(window[u][:].indirect(offsets[:, a // 16 : b // 16]), pairs[:, u, a:b])
 
         def group_wm(o, piece):
             ms = slice(piece * P // WM_PIECES, (piece + 1) * P // WM_PIECES)
             dst = wm_grouped[o][:, :, ms, :].rearrange("p s m d -> p m s d")
             src = wm_raw[:, o].rearrange("p d (m s) -> p m s d", s=PACK)[:, ms, :, :]
-            if o == D - 1:
+            if o == 0:
                 nc.scalar.copy(dst, src)
             else:
                 nc.gpsimd.tensor_scalar(dst, src, 1.0, 0.0, MULT, ADD)
 
         def quantize_wm(o):
-            tag = ("wm_codes0", "then_codes")[o]
-            wm_codes.append(keep.tile([P, N], U32, name="wm_codes%d" % o, tag=tag, align_bytes=64))
             nc.vector.quantize_mx(
                 out=wm_codes[o][:].bitcast(X4),
                 scales=wm_scales[o][:],
@@ -184,25 +168,11 @@ def tile_moe_mhm_gelu_kernel(
                 scatter(0, end - C, end)
                 if end <= HALF:
                     scatter(1, end - C, end)
-            if end == S - C:
-                for o in range(D):
-                    for piece in range(WM_PIECES):
-                        group_wm(o, piece)
-                quantize_wm(0)
-        scatter(1, HALF, S - P)
-        quantize_wm(1)
-        scatter(1, S - P, S)
-        spare = turn_pool.tile([P, N], F32, name="spare", tag="spare", bufs=1)
-        for warm_pass in range(WARM_PASSES):
-            nc.tensor.matmul_mx(
-                out=spare[:],
-                lhsT=wm_codes[1][:, 0:P].bitcast(X4),
-                lhsT_scale=wm_scales[1][:, 0:P],
-                rhs=wm_codes[1][:].bitcast(X4),
-                rhs_scale=wm_scales[1][:],
-                start=True,
-                stop=True,
-            )
+        for o in range(D):
+            for piece in range(WM_PIECES):
+                group_wm(o, piece)
+            quantize_wm(o)
+        scatter(1, HALF, S)
 
         c_grouped = [keep.tile([P, D, TC, 2], F32, name="c_grouped%d" % k, align_bytes=64) for k in range(CHUNKS)]
 
@@ -220,7 +190,7 @@ def tile_moe_mhm_gelu_kernel(
         out_words = out_1[0].rearrange("p t d -> p (t d)").bitcast(I32)
 
         for k in range(CHUNKS):
-            move = nc.vector.tensor_copy if k < CHUNKS // 2 else nc.scalar.copy
+            move = nc.vector.tensor_copy if k == 0 else nc.scalar.copy
             move(c_grouped[k][:, :, :, 1], window_cols(1, k))
             nc.vector.quantize_mx(
                 out=c_codes[k][:].bitcast(X4),

@@ -19,7 +19,6 @@ U16 = mybir.dt.uint16
 U8 = mybir.dt.uint8
 X4 = mybir.dt.float8_e4m3fn_x4
 GELU = mybir.ActivationFunctionType.Gelu_apprx_tanh
-COPY = mybir.ActivationFunctionType.Copy
 MULT = mybir.AluOpType.mult
 ADD = mybir.AluOpType.add
 
@@ -36,143 +35,202 @@ def tile_moe_mhm_gelu_kernel(
     with ExitStack() as ctx:
         keep = ctx.enter_context(tc.tile_pool(name="keep", bufs=1))
         ring = ctx.enter_context(tc.tile_pool(name="ring", bufs=3))
-        acc_pool = ctx.enter_context(tc.psum_pool(name="acc", bufs=2))
+        acc_pool = ctx.enter_context(tc.psum_pool(name="acc", bufs=3))
         turn_pool = ctx.enter_context(tc.psum_pool(name="turn", bufs=3))
 
         offsets = keep.tile([P, S // 16], U16, name="offsets")
-        xw = keep.tile([P, D * T], U32, name="xw", align_bytes=64)
-        xs = keep.tile([P, D * T], U8, name="xs", tag="then_words", align_bytes=64)
+        xs = keep.tile([P, D * T], U8, name="xs", align_bytes=64)
         ws = keep.tile([P, H], U8, name="ws", align_bytes=64)
-        w_first = keep.tile([P, H], U32, name="w_first", align_bytes=64)
-        ww = [w_first[:]]
+        ww = [keep.tile([P, H], U32, name="ww%d" % e, align_bytes=64) for e in range(E - 1)]
+        ww.append(keep.tile([P, H], U32, name="ww_last", tag="then_grouped1", align_bytes=64))
+        wm_raw = [keep.tile([P, PACK, N], F32, name="wm_raw%d" % o) for o in range(D)]
         gate_cols = keep.tile([P, TILES], F32, name="gate_cols")
         ident = keep.tile([P, P], F32, name="ident")
-        zero_in = keep.tile([P, 1], F32, name="zero_in", tag="then_w", align_bytes=64)
-        zero_bias = keep.tile([P, 1], F32, name="zero_bias", tag="then_wm", align_bytes=64)
+        zero_in = keep.tile([P, 1], F32, name="zero_in", tag="then_scales", align_bytes=64)
         zero = keep.tile([P, 1], F32, name="zero")
         gate_rows = keep.tile([P, P], F32, name="gate_rows")
 
-        nc.gpsimd.memset(xs[:].bitcast(I32), 0)
+        nc.vector.memset(xs[:].bitcast(I32), 0)
         nc.gpsimd.memset(ws[:].bitcast(I32), 0)
+        make_identity(nc, ident[:])
         nc.vector.memset(zero_in[:], 0.0)
-        nc.vector.memset(zero_bias[:], 0.0)
 
         nc.sync.dma_start(offsets[:], offs)
-        nc.sync.dma_start(
-            xw[:].bitcast(I32).rearrange("p (o t) -> p o t", o=D),
-            x_words.rearrange("o p t d -> p o (t d)").bitcast(I32),
-        )
         for q in range(QUADS):
             nc.sync.dma_start(
                 xs[32 * q : 32 * q + 4, :].bitcast(I32).rearrange("r (o t) -> r o t", o=D),
                 x_scales[:, 4 * q : 4 * q + 4, :].rearrange("o r t -> r o t").bitcast(I32),
             )
-        nc.scalar.activation(zero[:], zero_in[:], GELU, bias=zero_bias[:])
+        xw = keep.tile([P, D * T], U32, name="xw", align_bytes=64)
+        nc.sync.dma_start(
+            xw[:].bitcast(I32).rearrange("p (o t) -> p o t", o=D),
+            x_words.rearrange("o p t d -> p o (t d)").bitcast(I32),
+        )
+        nc.scalar.activation(zero[:], zero_in[:], GELU, bias=zero_in[:])
 
         def load_w(e):
-            nc.sync.dma_start(ww[e].bitcast(I32), w_words[e, 0].rearrange("p l d -> p (l d)").bitcast(I32))
+            nc.sync.dma_start(ww[e][:].bitcast(I32), w_words[e, 0].rearrange("p l d -> p (l d)").bitcast(I32))
 
         load_w(0)
+        nc.sync.dma_start(gate_rows[:], gate[0 : P // TILES, :].rearrange("a (j c) -> (a j) c", c=P))
         for q in range(QUADS):
             nc.sync.dma_start(
                 ws[32 * q : 32 * q + 4 * E, :].bitcast(I32),
                 w_scales[:, 0, 4 * q : 4 * q + 4, :].bitcast(I32),
             )
 
-        make_identity(nc, ident[:])
-        nc.sync.dma_start(gate_rows[:], gate[0 : P // TILES, :].rearrange("a (j c) -> (a j) c", c=P))
-        w_rest = keep.tile([P, (E - 1) * H], U32, name="w_rest", tag="then_w", align_bytes=64)
-        for e in range(1, E):
-            ww.append(w_rest[:, (e - 1) * H : e * H])
-            load_w(e)
+        load_w(1)
+        for o in range(D):
+            load_w(2 + o)
+            nc.sync.dma_start(wm_raw[o][:], wm[o * H : (o + 1) * H, :].rearrange("(p d) n -> p d n", d=PACK))
 
-        sg = keep.tile([P, S], U8, name="sg", align_bytes=64)
-        xg_first = keep.tile([P, HALF], U32, name="xg_first", align_bytes=64)
-        nc.vector.tensor_copy(xg_first[:], xw[:].indirect(offsets[:, : HALF // 16]))
-        nc.vector.tensor_copy(sg[:, :C], xs[:].indirect(offsets[:, : C // 16]))
-        nc.vector.tensor_copy(sg[:, C:], xs[:].indirect(offsets[:, C // 16 :]))
-        xg_rest = keep.tile([P, HALF], U32, name="xg_rest", tag="then_words", align_bytes=64)
-        nc.vector.tensor_copy(xg_rest[:], xw[:].indirect(offsets[:, HALF // 16 :]))
+        sg_first = keep.tile([P, HALF], U8, name="sg_first", align_bytes=64)
+        xg = keep.tile([P, S], U32, name="xg", align_bytes=64)
+        nc.vector.tensor_copy(sg_first[:], xs[:].indirect(offsets[:, : HALF // 16]))
+        for a, b in ((0, C), (C, HALF), (HALF, S)):
+            nc.vector.tensor_copy(xg[:, a:b], xw[:].indirect(offsets[:, a // 16 : b // 16]))
+        sg = [sg_first]
 
-        def gathered_words(j):
-            return (xg_first, xg_rest)[j * P // HALF][:, j * P % HALF : j * P % HALF + P]
+        def gathered_scales(j):
+            return sg[j * P // HALF][:, j * P % HALF : j * P % HALF + P]
 
         gate_turned = turn_pool.tile([P, 2, P], F32, name="turned")
         nc.tensor.transpose(gate_turned[:, 0, :], gate_rows[:], ident[:])
         nc.scalar.copy(gate_cols[:], gate_turned[:, 0, 0:TILES])
 
-        wm_raw = keep.tile([P, D, PACK, N], F32, name="wm_raw", tag="then_wm", align_bytes=64)
-        for o in range(D):
-            nc.sync.dma_start(wm_raw[:, o], wm[o * H : (o + 1) * H, :].rearrange("(p d) n -> p d n", d=PACK))
-
-        pairs = keep.tile([P, 2, S], F32, name="pairs")
+        pairs = keep.tile([P, 2, S], F32, name="pairs", tag="then_wm_codes1", align_bytes=64)
+        last_pairs = keep.tile([P, C], F32, name="last_pairs", tag="then_wm_codes0", align_bytes=64)
+        last_turned = []
         window = [keep.tile([P, D * T], F32, name="window%d" % u) for u in range(2)]
-        wm_grouped = [keep.tile([P, PACK, P, PACK], BF16, name="wm_grouped%d" % o, align_bytes=64) for o in range(D)]
-        wm_codes = [keep.tile([P, N], U32, name="wm_codes%d" % o, align_bytes=64) for o in range(D)]
+        wm_grouped = []
+        wm_codes = []
         wm_scales = [keep.tile([P, N], U8, name="wm_scales%d" % o, align_bytes=64) for o in range(D)]
 
-        def slot_tile(j):
+        accs = {}
+
+        def product(j):
             e = j * P // C
             cols = slice(j * P, (j + 1) * P)
             acc = acc_pool.tile([P, H], F32, name="acc")
+            accs[j] = acc
             nc.tensor.matmul_mx(
                 out=acc[:],
-                lhsT=gathered_words(j).bitcast(X4),
-                lhsT_scale=sg[:, cols],
-                rhs=ww[e].bitcast(X4),
+                lhsT=xg[:, cols].bitcast(X4),
+                lhsT_scale=gathered_scales(j),
+                rhs=ww[e][:].bitcast(X4),
                 rhs_scale=ws[4 * e : P, :],
                 start=True,
                 stop=True,
             )
-            y = ring.tile([P, 2, P, 2], F32, name="y")
-            nc.scalar.activation(y[:], acc[:].rearrange("s (p u i) -> s u p i", u=2, i=2), GELU, bias=zero[:])
-            c_slots = ring.tile([P, H], BF16, name="c_slots")
-            y_flat = y[:].rearrange("s u p i -> s (u p i)")
+
+        def slot_tile(j):
+            e = j * P // C
+            cols = slice(j * P, (j + 1) * P)
             if j == 0:
-                nc.scalar.activation(c_slots[:], y_flat, COPY, scale=gate_cols[:, j : j + 1])
-            else:
-                nc.gpsimd.tensor_scalar(c_slots[:], y_flat, gate_cols[:, j : j + 1], 0.0, MULT, ADD)
-            slot_pairs = c_slots[:].bitcast(F32)
+                product(0)
+                product(1)
+                product(2)
+            elif j > 2:
+                product(j)
+            acc = accs[j]
+            y = ring.tile([P, 2, P, 2], F32, name="y")
+            sums = acc[:].rearrange("s (p u i) -> s u p i", u=2, i=2)
+            gate_col = gate_cols[:, j : j + 1]
+            if j == 0:
+                for u in range(2):
+                    nc.scalar.activation(y[:, u], sums[:, u], GELU, bias=(zero_in, zero)[u][:])
+                    y_half = y[:, u].rearrange("s p i -> s (p i)")
+                    c_half = keep.tile([P, 2 * P], BF16, name="c_half%d" % u)
+                    if u == 0:
+                        nc.vector.tensor_scalar(c_half[:], y_half, gate_col, 0.0, MULT, ADD)
+                        sg.append(keep.tile([P, HALF], U8, name="sg_rest", tag="then_scales", align_bytes=64))
+                        nc.vector.tensor_copy(sg[1][:], xs[:].indirect(offsets[:, HALF // 16 :]))
+                    else:
+                        nc.gpsimd.tensor_scalar(c_half[:], y_half, gate_col, 0.0, MULT, ADD)
+                    turned = (acc_pool, turn_pool)[u].tile([P, 2, P], F32, name=("acc", "turned")[u])
+                    nc.tensor.transpose(turned[:, 0, :], c_half[:].bitcast(F32), ident[:])
+                    nc.scalar.copy(pairs[:, u, cols], turned[:, 0, :])
+                    scatter(u, 0, P)
+                return
+            c_slots = ring.tile([P, 2, 2 * P], BF16, name="c_slots")
+            nc.scalar.activation(y[:], sums, GELU, bias=zero[:])
+            nc.gpsimd.tensor_scalar(
+                c_slots[:].rearrange("s u k -> s (u k)"),
+                y[:].rearrange("s u p i -> s (u p i)"),
+                gate_col,
+                0.0,
+                MULT,
+                ADD,
+            )
+            if e == E - 1:
+                for u in range(2):
+                    if j % 2 == 0:
+                        last_turned.append(turn_pool.tile([P, 2, P], F32, name="turned"))
+                    nc.tensor.transpose(last_turned[u][:, j % 2, :], c_slots[:, u, :].bitcast(F32), ident[:])
+                if j % 2 == 1:
+                    nc.scalar.copy(last_pairs[:], last_turned[0][:].rearrange("p a b -> p (a b)"))
+                    nc.scalar.copy(pairs[:, 1, cols], last_turned[1][:, 1, :])
+                return
             turned = turn_pool.tile([P, 2, P], F32, name="turned")
             for u in range(2):
-                nc.tensor.transpose(turned[:, u, :], slot_pairs[:, u * P : (u + 1) * P], ident[:])
-            move = nc.vector.tensor_copy if j == 0 else nc.scalar.copy
-            move(pairs[:, :, cols], turned[:])
+                nc.tensor.transpose(turned[:, u, :], c_slots[:, u, :].bitcast(F32), ident[:])
+            nc.scalar.copy(pairs[:, :, cols], turned[:])
 
         def scatter(u, a, b):
-            nc.vector.tensor_copy(window[u][:].indirect(offsets[:, a // 16 : b // 16]), pairs[:, u, a:b])
+            src = last_pairs[:] if (u, a) == (0, S - C) else pairs[:, u, a:b]
+            nc.vector.tensor_copy(window[u][:].indirect(offsets[:, a // 16 : b // 16]), src)
 
         def group_wm(o, piece):
             ms = slice(piece * P // WM_PIECES, (piece + 1) * P // WM_PIECES)
             dst = wm_grouped[o][:, :, ms, :].rearrange("p s m d -> p m s d")
-            src = wm_raw[:, o].rearrange("p d (m s) -> p m s d", s=PACK)[:, ms, :, :]
-            if o == 0:
-                nc.scalar.copy(dst, src)
-            else:
-                nc.gpsimd.tensor_scalar(dst, src, 1.0, 0.0, MULT, ADD)
+            src = wm_raw[o][:].rearrange("p d (m s) -> p m s d", s=PACK)[:, ms, :, :]
+            nc.scalar.copy(dst, src)
 
         def quantize_wm(o):
+            wm_codes.append(
+                keep.tile([P, N], U32, name="wm_codes%d" % o, tag="then_wm_codes%d" % o, align_bytes=64)
+            )
             nc.vector.quantize_mx(
                 out=wm_codes[o][:].bitcast(X4),
                 scales=wm_scales[o][:],
                 in_=wm_grouped[o][:].rearrange("p s m d -> p (s m d)"),
             )
 
-        for j in range(TILES):
+        for j in (0, 1, 2, 3, 5, 4, 6, 7):
             slot_tile(j)
-            end = (j + 1) * P
-            if end <= C:
-                scatter(0, end - P, end)
-                scatter(1, end - P, end)
-            elif end % C == 0:
-                scatter(0, end - C, end)
-                if end <= HALF:
-                    scatter(1, end - C, end)
+            if j == 1:
+                scatter(0, P, C)
+                scatter(1, P, C)
+            if j == 3:
+                scatter(0, C, HALF)
+                scatter(1, C, HALF)
+            if j == 4:
+                scatter(0, HALF, S - C)
+                scatter(1, HALF, HALF + P)
+        scatter(0, S - C, S)
+        scatter(1, S - P, S)
         for o in range(D):
+            wm_grouped.append(
+                keep.tile(
+                    [P, PACK, P, PACK], BF16, name="wm_grouped%d" % o, tag="then_grouped%d" % o, align_bytes=64
+                )
+            )
             for piece in range(WM_PIECES):
                 group_wm(o, piece)
-            quantize_wm(o)
-        scatter(1, HALF, S)
+        quantize_wm(0)
+        nc.scalar.copy(pairs[:, 1, S - C : S - P], last_turned[1][:, 0, :])
+        scatter(1, HALF + P, S - P)
+        unread = turn_pool.tile([P, N], F32, name="turned")
+        for warm_up in range(4):
+            nc.tensor.matmul_mx(
+                out=unread[:],
+                lhsT=wm_codes[0][:, :P].bitcast(X4),
+                lhsT_scale=wm_scales[0][:, :P],
+                rhs=wm_codes[0][:].bitcast(X4),
+                rhs_scale=wm_scales[0][:],
+                start=True,
+                stop=True,
+            )
 
         c_grouped = [keep.tile([P, D, TC, 2], F32, name="c_grouped%d" % k, align_bytes=64) for k in range(CHUNKS)]
 
@@ -189,17 +247,24 @@ def tile_moe_mhm_gelu_kernel(
         out_rows = out_0.rearrange("(p s) t -> p s t", s=PACK)
         out_words = out_1[0].rearrange("p t d -> p (t d)").bitcast(I32)
 
-        for k in range(CHUNKS):
-            move = nc.vector.tensor_copy if k == 0 else nc.scalar.copy
-            move(c_grouped[k][:, :, :, 1], window_cols(1, k))
+        def quantize_c(k, heads):
             nc.vector.quantize_mx(
-                out=c_codes[k][:].bitcast(X4),
-                scales=c_scales[k][:],
-                in_=c_grouped[k][:].rearrange("p o t u -> p (o t u)").bitcast(BF16),
+                out=c_codes[k][:, heads.start * TC : heads.stop * TC].bitcast(X4),
+                scales=c_scales[k][:, heads.start * TC : heads.stop * TC],
+                in_=c_grouped[k][:, heads].rearrange("p o t u -> p (o t u)").bitcast(BF16),
             )
+
+        for k in range(CHUNKS):
+            move = nc.vector.tensor_copy if k in (0, 3,) else nc.scalar.copy
+            move(c_grouped[k][:, :, :, 1], window_cols(1, k))
+            if k == 0:
+                quantize_wm(1)
+            quantize_c(k, slice(0, D))
         for k in range(CHUNKS):
             cols = slice(k * TC, (k + 1) * TC)
-            merged = acc_pool.tile([P, PACK, TC], F32, name="merged", tag=("merged", "acc")[k // 2])
+            merged = acc_pool.tile(
+                [P, PACK, TC], F32, name="merged", tag=("merged", "acc")[k // 2], bufs=(2, 3)[k // 2]
+            )
             banks = [merged[:]]
             if k == CHUNKS - 1:
                 second = turn_pool.tile([P, PACK // 2, TC], F32, name="turned")

@@ -23,9 +23,11 @@ MULT = mybir.AluOpType.mult
 ADD = mybir.AluOpType.add
 
 HALF = S // 2
+RING = 3
 WM_PIECES = 4
 TC = 128
 CHUNKS = T // TC
+WARM_UPS = 4
 
 
 def tile_moe_mhm_gelu_kernel(
@@ -34,8 +36,8 @@ def tile_moe_mhm_gelu_kernel(
     nc = tc.nc
     with ExitStack() as ctx:
         keep = ctx.enter_context(tc.tile_pool(name="keep", bufs=1))
-        ring = ctx.enter_context(tc.tile_pool(name="ring", bufs=3))
-        acc_pool = ctx.enter_context(tc.psum_pool(name="acc", bufs=3))
+        ring = ctx.enter_context(tc.tile_pool(name="ring", bufs=RING))
+        acc_pool = ctx.enter_context(tc.psum_pool(name="acc", bufs=RING))
         turn_pool = ctx.enter_context(tc.psum_pool(name="turn", bufs=3))
 
         offsets = keep.tile([P, S // 16], U16, name="offsets")
@@ -48,24 +50,24 @@ def tile_moe_mhm_gelu_kernel(
         ident = keep.tile([P, P], F32, name="ident")
         zero_in = keep.tile([P, 1], F32, name="zero_in", tag="then_scales", align_bytes=64)
         zero = keep.tile([P, 1], F32, name="zero")
-        gate_rows = keep.tile([P, P], F32, name="gate_rows")
+        gate_rows = keep.tile([P, P], F32, name="gate_rows", tag="then_grouped0", align_bytes=64)
 
-        nc.vector.memset(xs[:].bitcast(I32), 0)
+        nc.gpsimd.memset(xs[:].bitcast(I32), 0)
         nc.gpsimd.memset(ws[:].bitcast(I32), 0)
         make_identity(nc, ident[:])
         nc.vector.memset(zero_in[:], 0.0)
 
         nc.sync.dma_start(offsets[:], offs)
-        for q in range(QUADS):
-            nc.sync.dma_start(
-                xs[32 * q : 32 * q + 4, :].bitcast(I32).rearrange("r (o t) -> r o t", o=D),
-                x_scales[:, 4 * q : 4 * q + 4, :].rearrange("o r t -> r o t").bitcast(I32),
-            )
         xw = keep.tile([P, D * T], U32, name="xw", align_bytes=64)
         nc.sync.dma_start(
             xw[:].bitcast(I32).rearrange("p (o t) -> p o t", o=D),
             x_words.rearrange("o p t d -> p o (t d)").bitcast(I32),
         )
+        for q in range(QUADS):
+            nc.sync.dma_start(
+                xs[32 * q : 32 * q + 4, :].bitcast(I32).rearrange("r (o t) -> r o t", o=D),
+                x_scales[:, 4 * q : 4 * q + 4, :].rearrange("o r t -> r o t").bitcast(I32),
+            )
         nc.scalar.activation(zero[:], zero_in[:], GELU, bias=zero_in[:])
 
         def load_w(e):
@@ -78,150 +80,131 @@ def tile_moe_mhm_gelu_kernel(
                 ws[32 * q : 32 * q + 4 * E, :].bitcast(I32),
                 w_scales[:, 0, 4 * q : 4 * q + 4, :].bitcast(I32),
             )
-
         load_w(1)
         for o in range(D):
-            load_w(2 + o)
+            load_w(E - D + o)
             nc.sync.dma_start(wm_raw[o][:], wm[o * H : (o + 1) * H, :].rearrange("(p d) n -> p d n", d=PACK))
 
-        sg_first = keep.tile([P, HALF], U8, name="sg_first", align_bytes=64)
-        xg = keep.tile([P, S], U32, name="xg", align_bytes=64)
-        nc.vector.tensor_copy(sg_first[:], xs[:].indirect(offsets[:, : HALF // 16]))
-        for a, b in ((0, C), (C, HALF), (HALF, S)):
-            nc.vector.tensor_copy(xg[:, a:b], xw[:].indirect(offsets[:, a // 16 : b // 16]))
-        sg = [sg_first]
+        sg = [keep.tile([P, HALF], U8, name="sg_first", align_bytes=64)]
+        xg = [keep.tile([P, HALF], U32, name="xg_first", align_bytes=64)]
+        nc.vector.tensor_copy(xg[0][:], xw[:].indirect(offsets[:, : HALF // 16]))
+        for a in range(0, HALF, C):
+            nc.vector.tensor_copy(sg[0][:, a : a + C], xs[:].indirect(offsets[:, a // 16 : (a + C) // 16]))
 
-        def gathered_scales(j):
-            return sg[j * P // HALF][:, j * P % HALF : j * P % HALF + P]
+        def gathered(halves, j):
+            return halves[j * P // HALF][:, j * P % HALF : j * P % HALF + P]
 
-        gate_turned = turn_pool.tile([P, 2, P], F32, name="turned")
-        nc.tensor.transpose(gate_turned[:, 0, :], gate_rows[:], ident[:])
-        nc.scalar.copy(gate_cols[:], gate_turned[:, 0, 0:TILES])
+        gate_turned = turn_pool.tile([P, P], F32, name="turned")
+        nc.tensor.transpose(gate_turned[:], gate_rows[:], ident[:])
+        nc.scalar.copy(gate_cols[:], gate_turned[:, 0:TILES])
+        xg.append(keep.tile([P, HALF], U32, name="xg_rest", tag="then_grouped0", align_bytes=64))
+        nc.vector.tensor_copy(xg[1][:], xw[:].indirect(offsets[:, HALF // 16 :]))
 
-        pairs = keep.tile([P, 2, S], F32, name="pairs", tag="then_wm_codes1", align_bytes=64)
-        last_pairs = keep.tile([P, C], F32, name="last_pairs", tag="then_wm_codes0", align_bytes=64)
-        last_turned = []
+        pairs = keep.tile([P, 2, S], F32, name="pairs", tag="then_codes1", align_bytes=64)
         window = [keep.tile([P, D * T], F32, name="window%d" % u) for u in range(2)]
-        wm_grouped = []
-        wm_codes = []
         wm_scales = [keep.tile([P, N], U8, name="wm_scales%d" % o, align_bytes=64) for o in range(D)]
-
-        accs = {}
+        sums = {}
 
         def product(j):
             e = j * P // C
-            cols = slice(j * P, (j + 1) * P)
             acc = acc_pool.tile([P, H], F32, name="acc")
-            accs[j] = acc
             nc.tensor.matmul_mx(
                 out=acc[:],
-                lhsT=xg[:, cols].bitcast(X4),
-                lhsT_scale=gathered_scales(j),
+                lhsT=gathered(xg, j).bitcast(X4),
+                lhsT_scale=gathered(sg, j),
                 rhs=ww[e][:].bitcast(X4),
                 rhs_scale=ws[4 * e : P, :],
                 start=True,
                 stop=True,
             )
+            sums[j] = acc[:].rearrange("s (p u i) -> s u p i", u=2, i=2)
 
-        def slot_tile(j):
-            e = j * P // C
-            cols = slice(j * P, (j + 1) * P)
-            if j == 0:
-                product(0)
-                product(1)
-                product(2)
-            elif j > 2:
-                product(j)
-            acc = accs[j]
+        def scatter(u, a, b):
+            nc.vector.tensor_copy(window[u][:].indirect(offsets[:, a // 16 : b // 16]), pairs[:, u, a:b])
+
+        def rounded_c(j):
             y = ring.tile([P, 2, P, 2], F32, name="y")
-            sums = acc[:].rearrange("s (p u i) -> s u p i", u=2, i=2)
-            gate_col = gate_cols[:, j : j + 1]
-            if j == 0:
-                for u in range(2):
-                    nc.scalar.activation(y[:, u], sums[:, u], GELU, bias=(zero_in, zero)[u][:])
-                    y_half = y[:, u].rearrange("s p i -> s (p i)")
-                    c_half = keep.tile([P, 2 * P], BF16, name="c_half%d" % u)
-                    if u == 0:
-                        nc.vector.tensor_scalar(c_half[:], y_half, gate_col, 0.0, MULT, ADD)
-                        sg.append(keep.tile([P, HALF], U8, name="sg_rest", tag="then_scales", align_bytes=64))
-                        nc.vector.tensor_copy(sg[1][:], xs[:].indirect(offsets[:, HALF // 16 :]))
-                    else:
-                        nc.gpsimd.tensor_scalar(c_half[:], y_half, gate_col, 0.0, MULT, ADD)
-                    turned = (acc_pool, turn_pool)[u].tile([P, 2, P], F32, name=("acc", "turned")[u])
-                    nc.tensor.transpose(turned[:, 0, :], c_half[:].bitcast(F32), ident[:])
-                    nc.scalar.copy(pairs[:, u, cols], turned[:, 0, :])
-                    scatter(u, 0, P)
-                return
             c_slots = ring.tile([P, 2, 2 * P], BF16, name="c_slots")
-            nc.scalar.activation(y[:], sums, GELU, bias=zero[:])
+            nc.scalar.activation(y[:], sums[j], GELU, bias=zero[:])
             nc.gpsimd.tensor_scalar(
                 c_slots[:].rearrange("s u k -> s (u k)"),
                 y[:].rearrange("s u p i -> s (u p i)"),
-                gate_col,
+                gate_cols[:, j : j + 1],
                 0.0,
                 MULT,
                 ADD,
             )
-            if e == E - 1:
-                for u in range(2):
-                    if j % 2 == 0:
-                        last_turned.append(turn_pool.tile([P, 2, P], F32, name="turned"))
-                    nc.tensor.transpose(last_turned[u][:, j % 2, :], c_slots[:, u, :].bitcast(F32), ident[:])
-                if j % 2 == 1:
-                    nc.scalar.copy(last_pairs[:], last_turned[0][:].rearrange("p a b -> p (a b)"))
-                    nc.scalar.copy(pairs[:, 1, cols], last_turned[1][:, 1, :])
-                return
-            turned = turn_pool.tile([P, 2, P], F32, name="turned")
+            return c_slots
+
+        for j in range(RING):
+            product(j)
+        y_first = ring.tile([P, 2, P, 2], F32, name="y")
+        for u in range(2):
+            nc.scalar.activation(y_first[:, u], sums[0][:, u], GELU, bias=(zero_in, zero)[u][:])
+            y_half = y_first[:, u].rearrange("s p i -> s (p i)")
+            c_half = keep.tile([P, 2 * P], BF16, name="c_half%d" % u)
+            (nc.vector, nc.gpsimd)[u].tensor_scalar(c_half[:], y_half, gate_cols[:, 0:1], 0.0, MULT, ADD)
+            if u == 0:
+                sg.append(keep.tile([P, HALF], U8, name="sg_rest", tag="then_scales", align_bytes=64))
+                nc.vector.tensor_copy(sg[1][:], xs[:].indirect(offsets[:, HALF // 16 :]))
+            turned_half = acc_pool.tile([P, P], F32, name="acc")
+            nc.tensor.transpose(turned_half[:], c_half[:].bitcast(F32), ident[:])
+            nc.scalar.copy(pairs[:, u, 0:P], turned_half[:])
+            scatter(u, 0, P)
+
+        last_first = TILES - C // P
+        for j in range(1, last_first):
+            c_slots = rounded_c(j)
+            product(j + RING - 1)
+            turned = acc_pool.tile([P, 2, P], F32, name="acc")
             for u in range(2):
                 nc.tensor.transpose(turned[:, u, :], c_slots[:, u, :].bitcast(F32), ident[:])
-            nc.scalar.copy(pairs[:, :, cols], turned[:])
+            nc.scalar.copy(pairs[:, :, j * P : (j + 1) * P], turned[:])
+            end = (j + 1) * P
+            if end <= HALF or end % C == 0:
+                for u in range(2):
+                    scatter(u, end - (P if end <= HALF else C), end)
 
-        def scatter(u, a, b):
-            src = last_pairs[:] if (u, a) == (0, S - C) else pairs[:, u, a:b]
-            nc.vector.tensor_copy(window[u][:].indirect(offsets[:, a // 16 : b // 16]), src)
+        last_turned = []
+        for j in range(last_first, TILES):
+            c_slots = rounded_c(j)
+            for u in range(2):
+                if j == last_first:
+                    last_turned.append(turn_pool.tile([P, 2, P], F32, name="turned"))
+                nc.tensor.transpose(last_turned[u][:, j - last_first, :], c_slots[:, u, :].bitcast(F32), ident[:])
+        nc.scalar.copy(pairs[:, 0, S - C :], last_turned[0][:].rearrange("p a b -> p (a b)"))
+        nc.scalar.copy(pairs[:, 1, S - C : S - P], last_turned[1][:, 0, :])
+        scatter(0, S - C, S)
+        scatter(1, S - C, S - P)
 
-        def group_wm(o, piece):
-            ms = slice(piece * P // WM_PIECES, (piece + 1) * P // WM_PIECES)
-            dst = wm_grouped[o][:, :, ms, :].rearrange("p s m d -> p m s d")
-            src = wm_raw[o][:].rearrange("p d (m s) -> p m s d", s=PACK)[:, ms, :, :]
-            nc.scalar.copy(dst, src)
-
-        def quantize_wm(o):
-            wm_codes.append(
-                keep.tile([P, N], U32, name="wm_codes%d" % o, tag="then_wm_codes%d" % o, align_bytes=64)
+        wm_grouped = []
+        for o in range(D):
+            wm_grouped.append(
+                keep.tile([P, PACK, P, PACK], BF16, name="wm_grouped%d" % o, tag="then_grouped%d" % o, align_bytes=64)
             )
+            for piece in range(WM_PIECES):
+                ms = slice(piece * P // WM_PIECES, (piece + 1) * P // WM_PIECES)
+                dst = wm_grouped[o][:, :, ms, :].rearrange("p s m d -> p m s d")
+                src = wm_raw[o][:].rearrange("p d (m s) -> p m s d", s=PACK)[:, ms, :, :]
+                if o == 0:
+                    nc.scalar.copy(dst, src)
+                else:
+                    nc.gpsimd.tensor_scalar(dst, src, 1.0, 0.0, MULT, ADD)
+
+        def quantize_wm(o, codes):
             nc.vector.quantize_mx(
-                out=wm_codes[o][:].bitcast(X4),
+                out=codes[:].bitcast(X4),
                 scales=wm_scales[o][:],
                 in_=wm_grouped[o][:].rearrange("p s m d -> p (s m d)"),
             )
 
-        for j in (0, 1, 2, 3, 5, 4, 6, 7):
-            slot_tile(j)
-            if j == 1:
-                scatter(0, P, C)
-                scatter(1, P, C)
-            if j == 3:
-                scatter(0, C, HALF)
-                scatter(1, C, HALF)
-            if j == 4:
-                scatter(0, HALF, S - C)
-                scatter(1, HALF, HALF + P)
-        scatter(0, S - C, S)
+        wm_codes = [keep.tile([P, N], U32, name="wm_codes0", align_bytes=64)]
+        quantize_wm(0, wm_codes[0])
+        nc.scalar.copy(pairs[:, 1, S - P :], last_turned[1][:, 1, :])
         scatter(1, S - P, S)
-        for o in range(D):
-            wm_grouped.append(
-                keep.tile(
-                    [P, PACK, P, PACK], BF16, name="wm_grouped%d" % o, tag="then_grouped%d" % o, align_bytes=64
-                )
-            )
-            for piece in range(WM_PIECES):
-                group_wm(o, piece)
-        quantize_wm(0)
-        nc.scalar.copy(pairs[:, 1, S - C : S - P], last_turned[1][:, 0, :])
-        scatter(1, HALF + P, S - P)
+
         unread = turn_pool.tile([P, N], F32, name="turned")
-        for warm_up in range(4):
+        for warm_up in range(WARM_UPS):
             nc.tensor.matmul_mx(
                 out=unread[:],
                 lhsT=wm_codes[0][:, :P].bitcast(X4),
@@ -233,12 +216,20 @@ def tile_moe_mhm_gelu_kernel(
             )
 
         c_grouped = [keep.tile([P, D, TC, 2], F32, name="c_grouped%d" % k, align_bytes=64) for k in range(CHUNKS)]
+        staged = {k: keep.tile([P, 2, D * TC], F32, name="staged%d" % k) for k in range(1, CHUNKS)}
 
         def window_cols(u, k):
             return window[u][:].rearrange("p (o t) -> p o t", o=D)[:, :, k * TC : (k + 1) * TC]
 
-        for k in range(CHUNKS):
-            nc.scalar.copy(c_grouped[k][:, :, :, 0], window_cols(0, k))
+        def stage(move, u, k):
+            move(staged[k][:, u, :].rearrange("p (o t) -> p o t", o=D), window_cols(u, k))
+
+        def weave(move, k):
+            move(c_grouped[k][:].rearrange("p o t u -> p (o t) u"), staged[k][:].rearrange("p u z -> p z u"))
+
+        nc.scalar.copy(c_grouped[0][:], window_cols(0, 0).unsqueeze(3).to_broadcast([P, D, TC, 2]))
+        for k in range(1, CHUNKS):
+            stage(nc.scalar.copy, 0, k)
 
         c_codes = [keep.tile([P, D * TC], U32, name="c_codes%d" % k, align_bytes=64) for k in range(CHUNKS)]
         c_scales = [keep.tile([P, D * TC], U8, name="c_scales%d" % k, align_bytes=64) for k in range(CHUNKS)]
@@ -247,26 +238,34 @@ def tile_moe_mhm_gelu_kernel(
         out_rows = out_0.rearrange("(p s) t -> p s t", s=PACK)
         out_words = out_1[0].rearrange("p t d -> p (t d)").bitcast(I32)
 
-        def quantize_c(k, heads):
+        def quantize_c(k):
             nc.vector.quantize_mx(
-                out=c_codes[k][:, heads.start * TC : heads.stop * TC].bitcast(X4),
-                scales=c_scales[k][:, heads.start * TC : heads.stop * TC],
-                in_=c_grouped[k][:, heads].rearrange("p o t u -> p (o t u)").bitcast(BF16),
+                out=c_codes[k][:].bitcast(X4),
+                scales=c_scales[k][:],
+                in_=c_grouped[k][:].rearrange("p o t u -> p (o t u)").bitcast(BF16),
             )
 
-        for k in range(CHUNKS):
-            move = nc.vector.tensor_copy if k in (0, 3,) else nc.scalar.copy
-            move(c_grouped[k][:, :, :, 1], window_cols(1, k))
-            if k == 0:
-                quantize_wm(1)
-            quantize_c(k, slice(0, D))
+        for k in range(1, CHUNKS, 2):
+            stage(nc.scalar.copy, 1, k)
+        for k in range(1, CHUNKS, 2):
+            weave(nc.scalar.copy, k)
+        nc.vector.tensor_copy(c_grouped[0][:, :, :, 1], window_cols(1, 0))
+        stage(nc.vector.tensor_copy, 1, 2)
+        wm_codes.append(keep.tile([P, N], U32, name="wm_codes1", tag="then_codes1", align_bytes=64))
+        quantize_wm(1, wm_codes[1])
+        quantize_c(0)
+        weave(nc.vector.tensor_copy, 2)
+        for k in range(1, CHUNKS):
+            quantize_c(k)
+
         for k in range(CHUNKS):
             cols = slice(k * TC, (k + 1) * TC)
-            merged = acc_pool.tile(
-                [P, PACK, TC], F32, name="merged", tag=("merged", "acc")[k // 2], bufs=(2, 3)[k // 2]
-            )
+            if k < 2:
+                merged = acc_pool.tile([P, PACK, TC], F32, name="merged", bufs=2)
+            else:
+                merged = acc_pool.tile([P, PACK, TC], F32, name="acc")
             banks = [merged[:]]
-            if k == CHUNKS - 1:
+            if k in (0, CHUNKS - 1):
                 second = turn_pool.tile([P, PACK // 2, TC], F32, name="turned")
                 banks = [merged[:, : PACK // 2, :], second[:]]
             per_bank = PACK // len(banks)
@@ -283,8 +282,12 @@ def tile_moe_mhm_gelu_kernel(
                     )
             result = keep.tile([P, PACK, TC], F32, name="result%d" % k)
             for i, bank in enumerate(banks):
-                nc.scalar.copy(result[:, i * per_bank : (i + 1) * per_bank, :], bank)
-            nc.sync.dma_start(out_rows[:, :, cols], result[:])
+                rows = slice(i * per_bank, (i + 1) * per_bank)
+                nc.scalar.copy(result[:, rows, :], bank)
+                if k == 0:
+                    nc.sync.dma_start(out_rows[:, rows, cols], result[:, rows, :])
+            if k > 0:
+                nc.sync.dma_start(out_rows[:, :, cols], result[:])
             rounded = keep.tile([P, TC, PACK], BF16, name="rounded%d" % k, align_bytes=64)
             nc.vector.tensor_copy(rounded[:], result[:].rearrange("p s t -> p t s"))
             nc.vector.quantize_mx(

@@ -1,7 +1,6 @@
 from contextlib import ExitStack
 
 import concourse.mybir as mybir
-from concourse.masks import make_identity
 
 D, T, E, C, H, N = 2, 512, 4, 256, 512, 512
 P = 128
@@ -27,6 +26,9 @@ RING = 3
 WM_PIECES = 4
 TC = 128
 CHUNKS = T // TC
+WW_AT = {1: 512, 2: 2560, 3: 20992}
+WM_RAW_AT = (4608, 12800)
+LAST = 3
 WARM_UPS = 4
 
 
@@ -36,45 +38,62 @@ def tile_moe_mhm_gelu_kernel(
     nc = tc.nc
     with ExitStack() as ctx:
         keep = ctx.enter_context(tc.tile_pool(name="keep", bufs=1))
+        shared = ctx.enter_context(tc.tile_pool(name="shared", bufs=1))
         ring = ctx.enter_context(tc.tile_pool(name="ring", bufs=RING))
         acc_pool = ctx.enter_context(tc.psum_pool(name="acc", bufs=RING))
         turn_pool = ctx.enter_context(tc.psum_pool(name="turn", bufs=3))
 
         offsets = keep.tile([P, S // 16], U16, name="offsets")
         xs = keep.tile([P, D * T], U8, name="xs", align_bytes=64)
-        ws = keep.tile([P, H], U8, name="ws", align_bytes=64)
-        ww = [keep.tile([P, H], U32, name="ww%d" % e, align_bytes=64) for e in range(E - 1)]
-        ww.append(keep.tile([P, H], U32, name="ww_last", tag="then_grouped1", align_bytes=64))
-        wm_raw = [keep.tile([P, PACK, N], F32, name="wm_raw%d" % o) for o in range(D)]
+        zeros = shared.tile([P, P], F32, name="zeros", offset=0, align_bytes=64)
+        draft = shared.tile([P, 7168], F32, name="draft", offset=512, align_bytes=64)
+        ws = shared.tile([P, H], U8, name="ws", offset=0, align_bytes=64)
+        ww = [keep.tile([P, H], U32, name="ww0", align_bytes=64)]
+        ww.extend(
+            shared.tile([P, H], U32, name="ww%d" % e, offset=WW_AT[e], align_bytes=64) for e in range(1, E)
+        )
+        wm_raw = [
+            shared.tile([P, PACK, N], F32, name="wm_raw%d" % o, offset=WM_RAW_AT[o], align_bytes=64) for o in range(D)
+        ]
         gate_cols = keep.tile([P, TILES], F32, name="gate_cols")
         ident = keep.tile([P, P], F32, name="ident")
         zero_in = keep.tile([P, 1], F32, name="zero_in", tag="then_scales", align_bytes=64)
         zero = keep.tile([P, 1], F32, name="zero")
-        gate_rows = keep.tile([P, P], F32, name="gate_rows", tag="then_grouped0", align_bytes=64)
+        gate_rows = keep.tile([P, P], F32, name="gate_rows")
 
         nc.gpsimd.memset(xs[:].bitcast(I32), 0)
+        nc.gpsimd.memset(zero_in[:], 0.0)
+        nc.gpsimd.memset(zeros[:], 0.0)
+        nc.gpsimd.affine_select(
+            out=draft[:, :P],
+            in_=zeros[:],
+            compare_op=mybir.AluOpType.not_equal,
+            fill=1.0,
+            base=0,
+            pattern=[[-1, P]],
+            channel_multiplier=1,
+        )
         nc.gpsimd.memset(ws[:].bitcast(I32), 0)
-        make_identity(nc, ident[:])
-        nc.vector.memset(zero_in[:], 0.0)
+        nc.gpsimd.tensor_copy(ident[:], draft[:, :P])
 
         nc.sync.dma_start(offsets[:], offs)
+        nc.scalar.dma_start(gate_rows[:], gate[0 : P // TILES, :].rearrange("a (j c) -> (a j) c", c=P))
         xw = keep.tile([P, D * T], U32, name="xw", align_bytes=64)
+        for q in range(QUADS):
+            (nc.sync, nc.scalar)[q // 2].dma_start(
+                xs[32 * q : 32 * q + 4, :].bitcast(I32).rearrange("r (o t) -> r o t", o=D),
+                x_scales[:, 4 * q : 4 * q + 4, :].rearrange("o r t -> r o t").bitcast(I32),
+            )
         nc.sync.dma_start(
             xw[:].bitcast(I32).rearrange("p (o t) -> p o t", o=D),
             x_words.rearrange("o p t d -> p o (t d)").bitcast(I32),
         )
-        for q in range(QUADS):
-            nc.sync.dma_start(
-                xs[32 * q : 32 * q + 4, :].bitcast(I32).rearrange("r (o t) -> r o t", o=D),
-                x_scales[:, 4 * q : 4 * q + 4, :].rearrange("o r t -> r o t").bitcast(I32),
-            )
         nc.scalar.activation(zero[:], zero_in[:], GELU, bias=zero_in[:])
 
         def load_w(e):
             nc.sync.dma_start(ww[e][:].bitcast(I32), w_words[e, 0].rearrange("p l d -> p (l d)").bitcast(I32))
 
         load_w(0)
-        nc.sync.dma_start(gate_rows[:], gate[0 : P // TILES, :].rearrange("a (j c) -> (a j) c", c=P))
         for q in range(QUADS):
             nc.sync.dma_start(
                 ws[32 * q : 32 * q + 4 * E, :].bitcast(I32),
@@ -86,23 +105,26 @@ def tile_moe_mhm_gelu_kernel(
             nc.sync.dma_start(wm_raw[o][:], wm[o * H : (o + 1) * H, :].rearrange("(p d) n -> p d n", d=PACK))
 
         sg = [keep.tile([P, HALF], U8, name="sg_first", align_bytes=64)]
-        xg = [keep.tile([P, HALF], U32, name="xg_first", align_bytes=64)]
-        nc.vector.tensor_copy(xg[0][:], xw[:].indirect(offsets[:, : HALF // 16]))
+        xg_first = [keep.tile([P, C], U32, name="xg_first%d" % e, align_bytes=64) for e in range(2)]
+        xg = [None]
+        nc.vector.tensor_copy(sg[0][:], xs[:].indirect(offsets[:, : HALF // 16]))
         for a in range(0, HALF, C):
-            nc.vector.tensor_copy(sg[0][:, a : a + C], xs[:].indirect(offsets[:, a // 16 : (a + C) // 16]))
+            nc.vector.tensor_copy(xg_first[a // C][:], xw[:].indirect(offsets[:, a // 16 : (a + C) // 16]))
 
         def gathered(halves, j):
+            if halves is xg and j * P < HALF:
+                return xg_first[j * P // C][:, j * P % C : j * P % C + P]
             return halves[j * P // HALF][:, j * P % HALF : j * P % HALF + P]
 
         gate_turned = turn_pool.tile([P, P], F32, name="turned")
         nc.tensor.transpose(gate_turned[:], gate_rows[:], ident[:])
         nc.scalar.copy(gate_cols[:], gate_turned[:, 0:TILES])
-        xg.append(keep.tile([P, HALF], U32, name="xg_rest", tag="then_grouped0", align_bytes=64))
+        xg.append(keep.tile([P, HALF], U32, name="xg_rest", align_bytes=64))
         nc.vector.tensor_copy(xg[1][:], xw[:].indirect(offsets[:, HALF // 16 :]))
 
-        pairs = keep.tile([P, 2, S], F32, name="pairs", tag="then_codes1", align_bytes=64)
+        pairs = keep.tile([P, 2, S], F32, name="pairs", align_bytes=64)
         window = [keep.tile([P, D * T], F32, name="window%d" % u) for u in range(2)]
-        wm_scales = [keep.tile([P, N], U8, name="wm_scales%d" % o, align_bytes=64) for o in range(D)]
+        wm_scales = [keep.tile([P, N], U8, name="wm_scales%d" % o, align_bytes=64) for o in range(2)]
         sums = {}
 
         def product(j):
@@ -152,7 +174,9 @@ def tile_moe_mhm_gelu_kernel(
             nc.scalar.copy(pairs[:, u, 0:P], turned_half[:])
             scatter(u, 0, P)
 
-        last_first = TILES - C // P
+        last_first = TILES - LAST
+        late = LAST * P
+        scatters = {1: [(0, 1, 1), (1, 1, 1)], 2: [(0, 2, 2), (1, 2, 2)], 4: [(0, 3, 4), (1, 3, 4)]}
         for j in range(1, last_first):
             c_slots = rounded_c(j)
             product(j + RING - 1)
@@ -160,48 +184,46 @@ def tile_moe_mhm_gelu_kernel(
             for u in range(2):
                 nc.tensor.transpose(turned[:, u, :], c_slots[:, u, :].bitcast(F32), ident[:])
             nc.scalar.copy(pairs[:, :, j * P : (j + 1) * P], turned[:])
-            end = (j + 1) * P
-            if end <= HALF or end % C == 0:
-                for u in range(2):
-                    scatter(u, end - (P if end <= HALF else C), end)
+            for u, a, b in scatters.get(j, ()):
+                scatter(u, a * P, (b + 1) * P)
 
         last_turned = []
         for j in range(last_first, TILES):
             c_slots = rounded_c(j)
+            if j + RING - 1 < TILES:
+                product(j + RING - 1)
             for u in range(2):
                 if j == last_first:
-                    last_turned.append(turn_pool.tile([P, 2, P], F32, name="turned"))
+                    last_turned.append(turn_pool.tile([P, LAST, P], F32, name="turned"))
                 nc.tensor.transpose(last_turned[u][:, j - last_first, :], c_slots[:, u, :].bitcast(F32), ident[:])
-        nc.scalar.copy(pairs[:, 0, S - C :], last_turned[0][:].rearrange("p a b -> p (a b)"))
-        nc.scalar.copy(pairs[:, 1, S - C : S - P], last_turned[1][:, 0, :])
-        scatter(0, S - C, S)
-        scatter(1, S - C, S - P)
+        nc.scalar.copy(pairs[:, 0, S - late :], last_turned[0][:].rearrange("p a b -> p (a b)"))
+        nc.scalar.copy(pairs[:, 1, S - late : S - C], last_turned[1][:, 0, :])
+        scatter(0, S - late, S)
+        scatter(1, S - late, S - C)
 
-        wm_grouped = []
-        for o in range(D):
-            wm_grouped.append(
-                keep.tile([P, PACK, P, PACK], BF16, name="wm_grouped%d" % o, tag="then_grouped%d" % o, align_bytes=64)
-            )
+        wm_grouped = shared.tile([P, PACK, D, P, PACK], BF16, name="wm_grouped", offset=WW_AT[E - 1], align_bytes=64)
+        for o in (1, 0):
             for piece in range(WM_PIECES):
                 ms = slice(piece * P // WM_PIECES, (piece + 1) * P // WM_PIECES)
-                dst = wm_grouped[o][:, :, ms, :].rearrange("p s m d -> p m s d")
+                dst = wm_grouped[:, :, o, ms, :].rearrange("p s m d -> p m s d")
                 src = wm_raw[o][:].rearrange("p d (m s) -> p m s d", s=PACK)[:, ms, :, :]
                 if o == 0:
                     nc.scalar.copy(dst, src)
                 else:
                     nc.gpsimd.tensor_scalar(dst, src, 1.0, 0.0, MULT, ADD)
 
-        def quantize_wm(o, codes):
+        def quantize_wm(h, codes):
             nc.vector.quantize_mx(
                 out=codes[:].bitcast(X4),
-                scales=wm_scales[o][:],
-                in_=wm_grouped[o][:].rearrange("p s m d -> p (s m d)"),
+                scales=wm_scales[h][:],
+                in_=wm_grouped[:, 2 * h : 2 * h + 2].rearrange("p s o m d -> p (s o m d)"),
             )
 
         wm_codes = [keep.tile([P, N], U32, name="wm_codes0", align_bytes=64)]
         quantize_wm(0, wm_codes[0])
-        nc.scalar.copy(pairs[:, 1, S - P :], last_turned[1][:, 1, :])
-        scatter(1, S - P, S)
+        pairs_last = shared.tile([P, C], F32, name="pairs_last", offset=WM_RAW_AT[1], align_bytes=64)
+        nc.scalar.copy(pairs_last[:], last_turned[1][:, 1:, :].rearrange("p a b -> p (a b)"))
+        nc.vector.tensor_copy(window[1][:].indirect(offsets[:, (S - C) // 16 :]), pairs_last[:])
 
         unread = turn_pool.tile([P, N], F32, name="turned")
         for warm_up in range(WARM_UPS):
@@ -215,81 +237,75 @@ def tile_moe_mhm_gelu_kernel(
                 stop=True,
             )
 
-        c_grouped = [keep.tile([P, D, TC, 2], F32, name="c_grouped%d" % k, align_bytes=64) for k in range(CHUNKS)]
-        staged = {k: keep.tile([P, 2, D * TC], F32, name="staged%d" % k) for k in range(1, CHUNKS)}
+        pieces = [(0, slice(o, o + 1)) for o in range(D)] + [(k, slice(0, D)) for k in range(1, CHUNKS)]
+        c_grouped, c_codes, c_scales = [], [], []
+        for i, (k, heads) in enumerate(pieces):
+            n_heads = heads.stop - heads.start
+            c_grouped.append(keep.tile([P, n_heads, TC, 2], F32, name="c_grouped%d" % i, align_bytes=64))
+            c_codes.append(keep.tile([P, n_heads * TC], U32, name="c_codes%d" % i, align_bytes=64))
+            c_scales.append(keep.tile([P, n_heads * TC], U8, name="c_scales%d" % i, align_bytes=64))
 
-        def window_cols(u, k):
-            return window[u][:].rearrange("p (o t) -> p o t", o=D)[:, :, k * TC : (k + 1) * TC]
+        def window_cols(u, i):
+            k, heads = pieces[i]
+            return window[u][:].rearrange("p (o t) -> p o t", o=D)[:, heads, k * TC : (k + 1) * TC]
 
-        def stage(move, u, k):
-            move(staged[k][:, u, :].rearrange("p (o t) -> p o t", o=D), window_cols(u, k))
+        for i in range(len(pieces)):
+            nc.scalar.copy(c_grouped[i][:], window_cols(0, i).unsqueeze(3).to_broadcast(list(c_grouped[i][:].shape)))
 
-        def weave(move, k):
-            move(c_grouped[k][:].rearrange("p o t u -> p (o t) u"), staged[k][:].rearrange("p u z -> p z u"))
-
-        nc.scalar.copy(c_grouped[0][:], window_cols(0, 0).unsqueeze(3).to_broadcast([P, D, TC, 2]))
-        for k in range(1, CHUNKS):
-            stage(nc.scalar.copy, 0, k)
-
-        c_codes = [keep.tile([P, D * TC], U32, name="c_codes%d" % k, align_bytes=64) for k in range(CHUNKS)]
-        c_scales = [keep.tile([P, D * TC], U8, name="c_scales%d" % k, align_bytes=64) for k in range(CHUNKS)]
         o_codes = keep.tile([P, T], U32, name="o_codes", align_bytes=64)
         o_scales = keep.tile([P, T], U8, name="o_scales", align_bytes=64)
         out_rows = out_0.rearrange("(p s) t -> p s t", s=PACK)
         out_words = out_1[0].rearrange("p t d -> p (t d)").bitcast(I32)
 
-        def quantize_c(k):
+        def weave(move, i):
+            move(c_grouped[i][:, :, :, 1], window_cols(1, i))
+
+        def quantize_c(i):
             nc.vector.quantize_mx(
-                out=c_codes[k][:].bitcast(X4),
-                scales=c_scales[k][:],
-                in_=c_grouped[k][:].rearrange("p o t u -> p (o t u)").bitcast(BF16),
+                out=c_codes[i][:].bitcast(X4),
+                scales=c_scales[i][:],
+                in_=c_grouped[i][:].rearrange("p o t u -> p (o t u)").bitcast(BF16),
             )
 
-        for k in range(1, CHUNKS, 2):
-            stage(nc.scalar.copy, 1, k)
-        for k in range(1, CHUNKS, 2):
-            weave(nc.scalar.copy, k)
-        nc.vector.tensor_copy(c_grouped[0][:, :, :, 1], window_cols(1, 0))
-        stage(nc.vector.tensor_copy, 1, 2)
-        wm_codes.append(keep.tile([P, N], U32, name="wm_codes1", tag="then_codes1", align_bytes=64))
-        quantize_wm(1, wm_codes[1])
+        weave(nc.scalar.copy, 2)
+        weave(nc.scalar.copy, 3)
+        weave(nc.vector.tensor_copy, 0)
+        weave(nc.vector.tensor_copy, 1)
         quantize_c(0)
-        weave(nc.vector.tensor_copy, 2)
-        for k in range(1, CHUNKS):
-            quantize_c(k)
+        quantize_c(1)
+        wm_codes.append(shared.tile([P, N], U32, name="wm_codes1", offset=WM_RAW_AT[1], align_bytes=64))
+        quantize_wm(1, wm_codes[1])
+        quantize_c(2)
+        weave(nc.vector.tensor_copy, 4)
+        quantize_c(3)
+        quantize_c(4)
 
-        for k in range(CHUNKS):
-            cols = slice(k * TC, (k + 1) * TC)
-            if k < 2:
-                merged = acc_pool.tile([P, PACK, TC], F32, name="merged", bufs=2)
-            else:
-                merged = acc_pool.tile([P, PACK, TC], F32, name="acc")
-            banks = [merged[:]]
-            if k in (0, CHUNKS - 1):
-                second = turn_pool.tile([P, PACK // 2, TC], F32, name="turned")
-                banks = [merged[:, : PACK // 2, :], second[:]]
-            per_bank = PACK // len(banks)
-            for s in range(PACK):
+        def c_operand(tiles, k, o):
+            return tiles[o][:] if k == 0 else tiles[k + 1][:, o * TC : (o + 1) * TC]
+
+        result = [keep.tile([P, PACK, TC], F32, name="result%d" % k) for k in range(CHUNKS)]
+
+        def merge(k, rows, bank, store):
+            for s in range(rows.start, rows.stop):
                 for o in range(D):
+                    w_cols = slice((s % 2 * D + o) * P, (s % 2 * D + o + 1) * P)
                     nc.tensor.matmul_mx(
-                        out=banks[s // per_bank][:, s % per_bank, :],
-                        lhsT=wm_codes[o][:, s * P : (s + 1) * P].bitcast(X4),
-                        lhsT_scale=wm_scales[o][:, s * P : (s + 1) * P],
-                        rhs=c_codes[k][:, o * TC : (o + 1) * TC].bitcast(X4),
-                        rhs_scale=c_scales[k][:, o * TC : (o + 1) * TC],
+                        out=bank[:, s - rows.start, :],
+                        lhsT=wm_codes[s // 2][:, w_cols].bitcast(X4),
+                        lhsT_scale=wm_scales[s // 2][:, w_cols],
+                        rhs=c_operand(c_codes, k, o).bitcast(X4),
+                        rhs_scale=c_operand(c_scales, k, o),
                         start=(o == 0),
                         stop=(o == D - 1),
                     )
-            result = keep.tile([P, PACK, TC], F32, name="result%d" % k)
-            for i, bank in enumerate(banks):
-                rows = slice(i * per_bank, (i + 1) * per_bank)
-                nc.scalar.copy(result[:, rows, :], bank)
-                if k == 0:
-                    nc.sync.dma_start(out_rows[:, rows, cols], result[:, rows, :])
-            if k > 0:
-                nc.sync.dma_start(out_rows[:, :, cols], result[:])
+            nc.scalar.copy(result[k][:, rows, :], bank[:])
+            if store is not None:
+                nc.sync.dma_start(out_rows[:, store, k * TC : (k + 1) * TC], result[k][:, store, :])
+
+        def planes(k):
+            cols = slice(k * TC, (k + 1) * TC)
             rounded = keep.tile([P, TC, PACK], BF16, name="rounded%d" % k, align_bytes=64)
-            nc.vector.tensor_copy(rounded[:], result[:].rearrange("p s t -> p t s"))
+            nc.vector.tensor_copy(rounded[:], result[k][:].rearrange("p s t -> p t s"))
             nc.vector.quantize_mx(
                 out=o_codes[:, cols].bitcast(X4),
                 scales=o_scales[:, cols],
@@ -298,6 +314,17 @@ def tile_moe_mhm_gelu_kernel(
             if k >= CHUNKS - 2:
                 done = slice(0, (k + 1) * TC) if k == CHUNKS - 2 else cols
                 nc.sync.dma_start(out_words[:, done], o_codes[:, done].bitcast(I32))
+
+        low, high, both = slice(0, 2), slice(2, 4), slice(0, 4)
+        for k in range(2):
+            merge(k, low, acc_pool.tile([P, 2, TC], F32, name="merged", bufs=2), low)
+            merge(k, high, acc_pool.tile([P, 2, TC], F32, name="acc"), high)
+            planes(k)
+        merge(2, both, acc_pool.tile([P, PACK, TC], F32, name="acc"), both)
+        planes(2)
+        merge(3, low, turn_pool.tile([P, 2, TC], F32, name="turned"), None)
+        merge(3, high, turn_pool.tile([P, 2, TC], F32, name="turned"), both)
+        planes(3)
         for q in range(QUADS):
             queue = nc.sync if q % 2 == 0 else nc.scalar
             queue.dma_start(

@@ -283,7 +283,9 @@ def tile_moe_mhm_gelu_kernel(
         def c_operand(tiles, k, o):
             return tiles[o][:] if k == 0 else tiles[k + 1][:, o * TC : (o + 1) * TC]
 
-        result = [keep.tile([P, PACK, TC], F32, name="result%d" % k) for k in range(CHUNKS)]
+        last_two = keep.tile([P, PACK, 2 * TC], F32, name="last_two")
+        result = [keep.tile([P, PACK, TC], F32, name="result%d" % k)[:] for k in range(2)]
+        result.extend([last_two[:, :, :TC], last_two[:, :, TC:]])
 
         def merge(k, rows, bank, store):
             for s in range(rows.start, rows.stop):
@@ -299,8 +301,10 @@ def tile_moe_mhm_gelu_kernel(
                         stop=(o == D - 1),
                     )
             nc.scalar.copy(result[k][:, rows, :], bank[:])
-            if store is not None:
-                nc.sync.dma_start(out_rows[:, store, k * TC : (k + 1) * TC], result[k][:, store, :])
+            if k < 2:
+                nc.sync.dma_start(out_rows[:, rows, k * TC : (k + 1) * TC], result[k][:, rows, :])
+            elif k == 3:
+                nc.sync.dma_start(out_rows[:, rows, 2 * TC :], last_two[:, rows, :])
 
         def planes(k):
             cols = slice(k * TC, (k + 1) * TC)

from contextlib import ExitStack

import concourse.mybir as mybir

D, T, E, C, H, N = 2, 512, 4, 256, 512, 512
P = 128
PACK = 4
QUADS = 4
S = E * C
TILES = S // P
FLOPS = 2 * H * H * S + 2 * D * H * N * T

F32 = mybir.dt.float32
BF16 = mybir.dt.bfloat16
I32 = mybir.dt.int32
U32 = mybir.dt.uint32
U16 = mybir.dt.uint16
U8 = mybir.dt.uint8
X4 = mybir.dt.float8_e4m3fn_x4
GELU = mybir.ActivationFunctionType.Gelu_apprx_tanh
MULT = mybir.AluOpType.mult
ADD = mybir.AluOpType.add

HALF = S // 2
RING = 3
WM_PIECES = 4
TC = 128
CHUNKS = T // TC
WW_AT = {1: 512, 2: 2560, 3: 20992}
WM_RAW_AT = (4608, 12800)
LAST = 3
WARM_UPS = 4


def tile_moe_mhm_gelu_kernel(
    tc, x_words, x_scales, w_words, w_scales, wm, gate, offs, out_0, out_1, out_2
):
    nc = tc.nc
    with ExitStack() as ctx:
        keep = ctx.enter_context(tc.tile_pool(name="keep", bufs=1))
        shared = ctx.enter_context(tc.tile_pool(name="shared", bufs=1))
        ring = ctx.enter_context(tc.tile_pool(name="ring", bufs=RING))
        acc_pool = ctx.enter_context(tc.psum_pool(name="acc", bufs=RING))
        turn_pool = ctx.enter_context(tc.psum_pool(name="turn", bufs=3))

        offsets = keep.tile([P, S // 16], U16, name="offsets")
        xs = keep.tile([P, D * T], U8, name="xs", align_bytes=64)
        zeros = shared.tile([P, P], F32, name="zeros", offset=0, align_bytes=64)
        draft = shared.tile([P, 7168], F32, name="draft", offset=512, align_bytes=64)
        ws = shared.tile([P, H], U8, name="ws", offset=0, align_bytes=64)
        ww = [keep.tile([P, H], U32, name="ww0", align_bytes=64)]
        ww.extend(
            shared.tile([P, H], U32, name="ww%d" % e, offset=WW_AT[e], align_bytes=64) for e in range(1, E)
        )
        wm_raw = [
            shared.tile([P, PACK, N], F32, name="wm_raw%d" % o, offset=WM_RAW_AT[o], align_bytes=64) for o in range(D)
        ]
        gate_cols = keep.tile([P, TILES], F32, name="gate_cols")
        ident = keep.tile([P, P], F32, name="ident")
        zero_in = keep.tile([P, 1], F32, name="zero_in", tag="then_scales", align_bytes=64)
        zero = keep.tile([P, 1], F32, name="zero")
        gate_rows = keep.tile([P, P], F32, name="gate_rows")

        nc.gpsimd.memset(xs[:].bitcast(I32), 0)
        nc.gpsimd.memset(zero_in[:], 0.0)
        nc.gpsimd.memset(zeros[:], 0.0)
        nc.gpsimd.affine_select(
            out=draft[:, :P],
            in_=zeros[:],
            compare_op=mybir.AluOpType.not_equal,
            fill=1.0,
            base=0,
            pattern=[[-1, P]],
            channel_multiplier=1,
        )
        nc.gpsimd.memset(ws[:].bitcast(I32), 0)
        nc.gpsimd.tensor_copy(ident[:], draft[:, :P])

        nc.sync.dma_start(offsets[:], offs)
        nc.scalar.dma_start(gate_rows[:], gate[0 : P // TILES, :].rearrange("a (j c) -> (a j) c", c=P))
        xw = keep.tile([P, D * T], U32, name="xw", align_bytes=64)
        for q in range(QUADS):
            (nc.sync, nc.scalar)[q // 2].dma_start(
                xs[32 * q : 32 * q + 4, :].bitcast(I32).rearrange("r (o t) -> r o t", o=D),
                x_scales[:, 4 * q : 4 * q + 4, :].rearrange("o r t -> r o t").bitcast(I32),
            )
        nc.sync.dma_start(
            xw[:].bitcast(I32).rearrange("p (o t) -> p o t", o=D),
            x_words.rearrange("o p t d -> p o (t d)").bitcast(I32),
        )
        nc.scalar.activation(zero[:], zero_in[:], GELU, bias=zero_in[:])

        def load_w(e):
            nc.sync.dma_start(ww[e][:].bitcast(I32), w_words[e, 0].rearrange("p l d -> p (l d)").bitcast(I32))

        load_w(0)
        for q in range(QUADS):
            nc.sync.dma_start(
                ws[32 * q : 32 * q + 4 * E, :].bitcast(I32),
                w_scales[:, 0, 4 * q : 4 * q + 4, :].bitcast(I32),
            )
        load_w(1)
        for o in range(D):
            load_w(E - D + o)
            nc.sync.dma_start(wm_raw[o][:], wm[o * H : (o + 1) * H, :].rearrange("(p d) n -> p d n", d=PACK))

        sg = [keep.tile([P, HALF], U8, name="sg_first", align_bytes=64)]
        xg_first = [keep.tile([P, C], U32, name="xg_first%d" % e, align_bytes=64) for e in range(2)]
        xg = [None]
        nc.vector.tensor_copy(sg[0][:], xs[:].indirect(offsets[:, : HALF // 16]))
        for a in range(0, HALF, C):
            nc.vector.tensor_copy(xg_first[a // C][:], xw[:].indirect(offsets[:, a // 16 : (a + C) // 16]))

        def gathered(halves, j):
            if halves is xg and j * P < HALF:
                return xg_first[j * P // C][:, j * P % C : j * P % C + P]
            return halves[j * P // HALF][:, j * P % HALF : j * P % HALF + P]

        gate_turned = turn_pool.tile([P, P], F32, name="turned")
        nc.tensor.transpose(gate_turned[:], gate_rows[:], ident[:])
        nc.scalar.copy(gate_cols[:], gate_turned[:, 0:TILES])
        xg.append(keep.tile([P, HALF], U32, name="xg_rest", align_bytes=64))
        nc.vector.tensor_copy(xg[1][:], xw[:].indirect(offsets[:, HALF // 16 :]))

        pairs = keep.tile([P, 2, S], F32, name="pairs", align_bytes=64)
        window = [keep.tile([P, D * T], F32, name="window%d" % u) for u in range(2)]
        wm_scales = [keep.tile([P, N], U8, name="wm_scales%d" % o, align_bytes=64) for o in range(2)]
        sums = {}

        def product(j):
            e = j * P // C
            acc = acc_pool.tile([P, H], F32, name="acc")
            nc.tensor.matmul_mx(
                out=acc[:],
                lhsT=gathered(xg, j).bitcast(X4),
                lhsT_scale=gathered(sg, j),
                rhs=ww[e][:].bitcast(X4),
                rhs_scale=ws[4 * e : P, :],
                start=True,
                stop=True,
            )
            sums[j] = acc[:].rearrange("s (p u i) -> s u p i", u=2, i=2)

        def scatter(u, a, b):
            nc.vector.tensor_copy(window[u][:].indirect(offsets[:, a // 16 : b // 16]), pairs[:, u, a:b])

        def rounded_c(j):
            y = ring.tile([P, 2, P, 2], F32, name="y")
            c_slots = ring.tile([P, 2, 2 * P], BF16, name="c_slots")
            nc.scalar.activation(y[:], sums[j], GELU, bias=zero[:])
            nc.gpsimd.tensor_scalar(
                c_slots[:].rearrange("s u k -> s (u k)"),
                y[:].rearrange("s u p i -> s (u p i)"),
                gate_cols[:, j : j + 1],
                0.0,
                MULT,
                ADD,
            )
            return c_slots

        for j in range(RING):
            product(j)
        y_first = ring.tile([P, 2, P, 2], F32, name="y")
        for u in range(2):
            nc.scalar.activation(y_first[:, u], sums[0][:, u], GELU, bias=(zero_in, zero)[u][:])
            y_half = y_first[:, u].rearrange("s p i -> s (p i)")
            c_half = keep.tile([P, 2 * P], BF16, name="c_half%d" % u)
            (nc.vector, nc.gpsimd)[u].tensor_scalar(c_half[:], y_half, gate_cols[:, 0:1], 0.0, MULT, ADD)
            if u == 0:
                sg.append(keep.tile([P, HALF], U8, name="sg_rest", tag="then_scales", align_bytes=64))
                nc.vector.tensor_copy(sg[1][:], xs[:].indirect(offsets[:, HALF // 16 :]))
            turned_half = acc_pool.tile([P, P], F32, name="acc")
            nc.tensor.transpose(turned_half[:], c_half[:].bitcast(F32), ident[:])
            nc.scalar.copy(pairs[:, u, 0:P], turned_half[:])
            scatter(u, 0, P)

        last_first = TILES - LAST
        late = LAST * P
        scatters = {1: [(0, 1, 1), (1, 1, 1)], 2: [(0, 2, 2), (1, 2, 2)], 4: [(0, 3, 4), (1, 3, 4)]}
        for j in range(1, last_first):
            c_slots = rounded_c(j)
            product(j + RING - 1)
            turned = acc_pool.tile([P, 2, P], F32, name="acc")
            for u in range(2):
                nc.tensor.transpose(turned[:, u, :], c_slots[:, u, :].bitcast(F32), ident[:])
            nc.scalar.copy(pairs[:, :, j * P : (j + 1) * P], turned[:])
            for u, a, b in scatters.get(j, ()):
                scatter(u, a * P, (b + 1) * P)

        last_turned = []
        for j in range(last_first, TILES):
            c_slots = rounded_c(j)
            if j + RING - 1 < TILES:
                product(j + RING - 1)
            for u in range(2):
                if j == last_first:
                    last_turned.append(turn_pool.tile([P, LAST, P], F32, name="turned"))
                nc.tensor.transpose(last_turned[u][:, j - last_first, :], c_slots[:, u, :].bitcast(F32), ident[:])
        nc.scalar.copy(pairs[:, 0, S - late :], last_turned[0][:].rearrange("p a b -> p (a b)"))
        nc.scalar.copy(pairs[:, 1, S - late : S - C], last_turned[1][:, 0, :])
        scatter(0, S - late, S)
        scatter(1, S - late, S - C)

        wm_grouped = shared.tile([P, PACK, D, P, PACK], BF16, name="wm_grouped", offset=WW_AT[E - 1], align_bytes=64)
        for o in (1, 0):
            for piece in range(WM_PIECES):
                ms = slice(piece * P // WM_PIECES, (piece + 1) * P // WM_PIECES)
                dst = wm_grouped[:, :, o, ms, :].rearrange("p s m d -> p m s d")
                src = wm_raw[o][:].rearrange("p d (m s) -> p m s d", s=PACK)[:, ms, :, :]
                if o == 0:
                    nc.scalar.copy(dst, src)
                else:
                    nc.gpsimd.tensor_scalar(dst, src, 1.0, 0.0, MULT, ADD)

        def quantize_wm(h, codes):
            nc.vector.quantize_mx(
                out=codes[:].bitcast(X4),
                scales=wm_scales[h][:],
                in_=wm_grouped[:, 2 * h : 2 * h + 2].rearrange("p s o m d -> p (s o m d)"),
            )

        wm_codes = [keep.tile([P, N], U32, name="wm_codes0", align_bytes=64)]
        quantize_wm(0, wm_codes[0])
        pairs_last = shared.tile([P, C], F32, name="pairs_last", offset=WM_RAW_AT[1], align_bytes=64)
        nc.scalar.copy(pairs_last[:], last_turned[1][:, 1:, :].rearrange("p a b -> p (a b)"))
        nc.vector.tensor_copy(window[1][:].indirect(offsets[:, (S - C) // 16 :]), pairs_last[:])

        unread = turn_pool.tile([P, N], F32, name="turned")
        for warm_up in range(WARM_UPS):
            nc.tensor.matmul_mx(
                out=unread[:],
                lhsT=wm_codes[0][:, :P].bitcast(X4),
                lhsT_scale=wm_scales[0][:, :P],
                rhs=wm_codes[0][:].bitcast(X4),
                rhs_scale=wm_scales[0][:],
                start=True,
                stop=True,
            )

        pieces = [(0, slice(o, o + 1)) for o in range(D)] + [(k, slice(0, D)) for k in range(1, CHUNKS)]
        c_grouped, c_codes, c_scales = [], [], []
        for i, (k, heads) in enumerate(pieces):
            n_heads = heads.stop - heads.start
            c_grouped.append(keep.tile([P, n_heads, TC, 2], F32, name="c_grouped%d" % i, align_bytes=64))
            c_codes.append(keep.tile([P, n_heads * TC], U32, name="c_codes%d" % i, align_bytes=64))
            c_scales.append(keep.tile([P, n_heads * TC], U8, name="c_scales%d" % i, align_bytes=64))

        def window_cols(u, i):
            k, heads = pieces[i]
            return window[u][:].rearrange("p (o t) -> p o t", o=D)[:, heads, k * TC : (k + 1) * TC]

        for i in range(len(pieces)):
            nc.scalar.copy(c_grouped[i][:], window_cols(0, i).unsqueeze(3).to_broadcast(list(c_grouped[i][:].shape)))

        o_codes = keep.tile([P, T], U32, name="o_codes", align_bytes=64)
        o_scales = keep.tile([P, T], U8, name="o_scales", align_bytes=64)
        out_rows = out_0.rearrange("(p s) t -> p s t", s=PACK)
        out_words = out_1[0].rearrange("p t d -> p (t d)").bitcast(I32)

        def weave(move, i):
            move(c_grouped[i][:, :, :, 1], window_cols(1, i))

        def quantize_c(i):
            nc.vector.quantize_mx(
                out=c_codes[i][:].bitcast(X4),
                scales=c_scales[i][:],
                in_=c_grouped[i][:].rearrange("p o t u -> p (o t u)").bitcast(BF16),
            )

        weave(nc.scalar.copy, 2)
        weave(nc.scalar.copy, 3)
        weave(nc.vector.tensor_copy, 0)
        weave(nc.vector.tensor_copy, 1)
        quantize_c(0)
        quantize_c(1)
        wm_codes.append(shared.tile([P, N], U32, name="wm_codes1", offset=WM_RAW_AT[1], align_bytes=64))
        quantize_wm(1, wm_codes[1])
        quantize_c(2)
        weave(nc.vector.tensor_copy, 4)
        quantize_c(3)
        quantize_c(4)

        def c_operand(tiles, k, o):
            return tiles[o][:] if k == 0 else tiles[k + 1][:, o * TC : (o + 1) * TC]

        last_two = keep.tile([P, PACK, 2 * TC], F32, name="last_two")
        result = [keep.tile([P, PACK, TC], F32, name="result%d" % k)[:] for k in range(2)]
        result.extend([last_two[:, :, :TC], last_two[:, :, TC:]])

        def merge(k, rows, bank, store):
            for s in range(rows.start, rows.stop):
                for o in range(D):
                    w_cols = slice((s % 2 * D + o) * P, (s % 2 * D + o + 1) * P)
                    nc.tensor.matmul_mx(
                        out=bank[:, s - rows.start, :],
                        lhsT=wm_codes[s // 2][:, w_cols].bitcast(X4),
                        lhsT_scale=wm_scales[s // 2][:, w_cols],
                        rhs=c_operand(c_codes, k, o).bitcast(X4),
                        rhs_scale=c_operand(c_scales, k, o),
                        start=(o == 0),
                        stop=(o == D - 1),
                    )
            nc.scalar.copy(result[k][:, rows, :], bank[:])
            if k < 2:
                nc.sync.dma_start(out_rows[:, rows, k * TC : (k + 1) * TC], result[k][:, rows, :])
            elif k == 3:
                nc.sync.dma_start(out_rows[:, rows, 2 * TC :], last_two[:, rows, :])

        def planes(k):
            cols = slice(k * TC, (k + 1) * TC)
            rounded = keep.tile([P, TC, PACK], BF16, name="rounded%d" % k, align_bytes=64)
            nc.vector.tensor_copy(rounded[:], result[k][:].rearrange("p s t -> p t s"))
            nc.vector.quantize_mx(
                out=o_codes[:, cols].bitcast(X4),
                scales=o_scales[:, cols],
                in_=rounded[:].rearrange("p t s -> p (t s)"),
            )
            if k >= CHUNKS - 2:
                done = slice(0, (k + 1) * TC) if k == CHUNKS - 2 else cols
                nc.sync.dma_start(out_words[:, done], o_codes[:, done].bitcast(I32))

        low, high, both = slice(0, 2), slice(2, 4), slice(0, 4)
        for k in range(2):
            merge(k, low, acc_pool.tile([P, 2, TC], F32, name="merged", bufs=2), low)
            merge(k, high, acc_pool.tile([P, 2, TC], F32, name="acc"), high)
            planes(k)
        merge(2, both, acc_pool.tile([P, PACK, TC], F32, name="acc"), both)
        planes(2)
        merge(3, low, turn_pool.tile([P, 2, TC], F32, name="turned"), None)
        merge(3, high, turn_pool.tile([P, 2, TC], F32, name="turned"), both)
        planes(3)
        for q in range(QUADS):
            queue = nc.sync if q % 2 == 0 else nc.scalar
            queue.dma_start(
                out_2[0, 4 * q : 4 * q + 4, :].bitcast(I32), o_scales[32 * q : 32 * q + 4, :].bitcast(I32)
            )
